import numpy as np
import ml_dtypes


def mxq(x, axis, fmt="e4m3"):
    dtype, down = {"e4m3": (ml_dtypes.float8_e4m3fn, 7), "e5m2": (ml_dtypes.float8_e5m2, 14)}[fmt]
    v = np.moveaxis(np.asarray(x, np.float32).astype(ml_dtypes.bfloat16).astype(np.float64), axis, -1)
    blocks = v.reshape(v.shape[:-1] + (-1, 32))
    amax = np.abs(blocks).max(-1, keepdims=True)
    byte = np.maximum(np.where(amax > 0, np.frexp(amax)[1] - 1 + 127, 0) - down, 1)
    scale = np.exp2(byte - 127.0)
    codes = (blocks / scale).astype(np.float32).astype(dtype).astype(np.float64)
    return np.moveaxis((codes * scale).reshape(v.shape), -1, axis)


WIDE = False


def mx_kscale(k):
    if not WIDE:
        return np.ones(k)
    levels = np.array([10, -10, 5, -5, 0])
    if k % 512:
        return np.exp2(np.random.permutation(np.resize(levels, k // 32))).repeat(32)
    a = np.empty((k // 512, 16))
    for p in range(k // 512):
        a[p, :8] = np.random.permutation(np.resize(levels, 8))
        for g in range(8):
            far = levels[np.abs(levels - a[p, g]) >= 10]
            a[p, g + 8] = far[np.random.randint(len(far))]
    return np.exp2(a.ravel()).repeat(32)


def f64(x):
    return np.asarray(x).astype(np.float64)


def striped(idx):
    return np.tile(np.asarray(idx).reshape(-1, 16).T, (8, 1)).astype(np.uint16)


def unstriped(offs):
    return offs[:16].T.reshape(-1).astype(np.int64)


E2M1 = np.array([0.0, 0.5, 1.0, 1.5, 2.0, 3.0, 4.0, 6.0, -0.0, -0.5, -1.0, -1.5, -2.0, -3.0, -4.0, -6.0])


def pack_weight(w, fmt):
    k, n = w.shape
    w = f64(np.asarray(w, np.float32).astype(ml_dtypes.bfloat16)).reshape(k // 32, 32, n)
    amax = np.abs(w).max(1)
    if fmt == "e4m3":
        byte = np.frexp(amax)[1] - 1 + 127 - 7
    else:
        mant, ex = np.frexp(amax / 6.0)
        byte = np.where(mant > 0.5, ex, ex - 1) + 127
    byte = np.clip(np.where(amax > 0, byte, 1), 1, 254)
    scaled = (w * np.exp2(127.0 - byte)[:, None, :]).reshape(k, n).astype(np.float32)
    by_word = np.ascontiguousarray(scaled.reshape(k // 512, 128, 4, n).transpose(0, 1, 3, 2))
    if fmt == "e4m3":
        words = by_word.astype(ml_dtypes.float8_e4m3fn).view(np.uint8)
    else:
        c = by_word.astype(ml_dtypes.float4_e2m1fn).view(np.uint8) & 0xF
        words = (c[..., 0::2] | (c[..., 1::2] << 4)).reshape(k // 512, 128, 2 * n)
    return np.ascontiguousarray(words), np.ascontiguousarray(byte.astype(np.uint8).reshape(k // 512, 16, n))


def unpack_weight(words, scales, fmt):
    g, _, n = scales.shape
    words = np.ascontiguousarray(words).reshape(g, 128, n, -1)
    if fmt == "e4m3":
        vals = words.view(ml_dtypes.float8_e4m3fn).astype(np.float64)
    else:
        nib = np.empty((g, 128, n, 4), np.uint8)
        nib[..., 0::2] = words & 0xF
        nib[..., 1::2] = words >> 4
        vals = E2M1[nib]
    vals = vals * np.repeat(np.exp2(scales.astype(np.float64) - 127.0), 8, axis=1)[..., None]
    return vals.transpose(0, 1, 3, 2).reshape(g * 512, n)


D, T, I, Q, E = 512, 2048, 1024, 128, 512


def setup_inputs():
    n = np.random.standard_normal
    idx = (np.random.randint(0, T // 64, I // 64)[:, None] * 64 + np.arange(64)).reshape(-1)
    fd = mx_kscale(D)
    fi = mx_kscale(I)
    keysp = pack_weight(n((D, T)) / fd[:, None], "e4m3")
    return {
        "query": (n((D, Q)) * 0.4 / np.sqrt(D) * fd[:, None]).astype(np.float32),
        "keys_words": keysp[0],
        "keys_scales": keysp[1],
        "mask": (np.where(np.random.uniform(size=(Q, I)) < 0.5, 0.0, -30.0)).astype(np.float32),
        "size": (np.random.uniform(0.5, 2.0, (1, I)) * fi).astype(np.float32),
        "vsc": (np.random.uniform(0.5, 2.0, (I, 1)) / fi[:, None]).astype(np.float32),
        "vals": (n((E, T))).astype(np.float32),
        "offs": striped(idx),
    }


def reference(query, keys_words, keys_scales, mask, size, vsc, vals, offs):
    idx = unstriped(offs)
    keysu = unpack_weight(keys_words, keys_scales, "e4m3")
    queryq = mxq(f64(query), 0, "e4m3")
    keysidxg = keysu[:, idx]
    a = queryq.T @ keysidxg
    s = a + f64(mask)
    p = np.exp(s - np.max(s, axis=1, keepdims=True))
    w = p * f64(size) / np.sum(p, axis=1, keepdims=True)
    wt = w.T
    vt = f64(vals)[:, idx].T
    vv = vt * f64(vsc)
    wtq = mxq(wt, 0, "e4m3")
    vvq = mxq(vv, 0, "e4m3")
    o = wtq.T @ vvq
    return o

@@ -1,0 +1,203 @@
+from contextlib import ExitStack
+
+import concourse.mybir as mybir
+from concourse.masks import make_identity
+
+D, T, I, Q, E = 512, 2048, 1024, 128, 512
+FLOPS = 2 * Q * I * D + 2 * Q * I * E
+
+F32 = mybir.dt.float32
+BF16 = mybir.dt.bfloat16
+I32 = mybir.dt.int32
+U32 = mybir.dt.uint32
+U16 = mybir.dt.uint16
+U8 = mybir.dt.uint8
+FP8X4 = mybir.dt.float8_e4m3fn_x4
+ALU = mybir.AluOpType
+ACT = mybir.ActivationFunctionType
+AX = mybir.AxisListType
+
+P = 128
+PACK = 4
+KP = P * PACK
+PASSES = I // KP
+BLOCKS = E // P
+COLS = KP // 16
+ON_VECTOR = [(3, 1)]
+
+
+def tile_attend_beamcache_kernel(tc, query, keys_words, keys_scales, mask, size, vsc, vals, offs, out):
+    nc = tc.nc
+    with ExitStack() as ctx:
+        keep = ctx.enter_context(tc.tile_pool(name="keep", bufs=1))
+        ring = ctx.enter_context(tc.tile_pool(name="ring", bufs=3))
+        psum = ctx.enter_context(tc.psum_pool(name="psum", bufs=2))
+        psum_v = ctx.enter_context(tc.psum_pool(name="psum_v", bufs=4))
+
+        offsets = keep.tile([P, I // 16], U16, name="offsets")
+        nc.sync.dma_start(offsets[:], offs)
+
+        ks_pool = keep.tile([P, T], U8, name="ks_pool", align_bytes=64)
+        nc.gpsimd.memset(ks_pool[:].bitcast(I32), 0)
+        for quad in range(4):
+            nc.scalar.dma_start(
+                ks_pool[32 * quad : 32 * quad + 4, :].bitcast(I32),
+                keys_scales[0, 4 * quad : 4 * quad + 4, :].bitcast(I32),
+            )
+        kw_pool = keep.tile([P, T], I32, name="kw_pool", align_bytes=64)
+        nc.sync.dma_start(kw_pool[:], keys_words[0].rearrange("p n t -> p (n t)").bitcast(I32))
+        q_raw = keep.tile([P, PACK, Q], F32, name="q_raw")
+        nc.sync.dma_start(q_raw[:], query.rearrange("(p j) q -> p j q", j=PACK))
+        v_pool = [keep.tile([P, T], F32, name="v_pool%d" % b, align_bytes=64) for b in range(BLOCKS)]
+        nc.sync.dma_start(v_pool[0][:], vals[0:P, :])
+        mask_sb = keep.tile([P, I], F32, name="mask_sb")
+        nc.sync.dma_start(mask_sb[:], mask)
+        for b in range(1, BLOCKS):
+            nc.sync.dma_start(v_pool[b][:], vals[b * P : (b + 1) * P, :])
+
+        size_col = keep.tile([P, PASSES, PACK], F32, name="size_col")
+        nc.scalar.dma_start(size_col[:], size.rearrange("o (g p t) -> p (o g) t", g=PASSES, t=PACK))
+        vsc_col = keep.tile([P, PASSES, PACK], F32, name="vsc_col")
+        nc.scalar.dma_start(vsc_col[:], vsc.rearrange("(g p t) o -> p g (t o)", g=PASSES, t=PACK))
+        ident = keep.tile([P, P], F32, name="ident")
+        make_identity(nc, ident[:])
+
+        ks = keep.tile([P, I], U8, name="ks", align_bytes=64)
+        nc.vector.tensor_copy(ks[:], ks_pool[:].indirect(offsets[:]))
+        kw = keep.tile([P, I], U32, name="kw", align_bytes=64)
+        nc.vector.tensor_copy(kw[:], kw_pool[:].bitcast(U32).indirect(offsets[:]))
+
+        q_bf = keep.tile([P, Q, PACK], BF16, name="q_bf", align_bytes=64)
+        nc.scalar.copy(q_bf[:], q_raw[:].rearrange("p j q -> p q j"))
+        q_codes = keep.tile([P, Q], U32, name="q_codes", align_bytes=64)
+        q_scales = keep.tile([P, Q], U8, name="q_scales", align_bytes=64)
+        nc.vector.quantize_mx(out=q_codes[:].bitcast(FP8X4), scales=q_scales[:], in_=q_bf[:].rearrange("p q j -> p (q j)"))
+
+        size_ps = []
+        for g in range(PASSES):
+            bank = psum.tile([P, PACK, P], F32, name="size_ps%d" % g, tag="late")
+            for t in range(PACK):
+                nc.tensor.transpose(bank[:, t, :], size_col[:, g, t : t + 1].to_broadcast([P, P]), ident[:])
+            size_ps.append(bank)
+
+        score_ps = []
+        for g in range(PASSES):
+            cols = slice(g * KP, (g + 1) * KP)
+            bank = psum.tile([P, KP], F32, name="score_ps%d" % g, tag="early")
+            nc.tensor.matmul_mx(
+                out=bank[:], lhsT=q_codes[:].bitcast(FP8X4), lhsT_scale=q_scales[:],
+                rhs=kw[:, cols].bitcast(FP8X4), rhs_scale=ks[:, cols], start=True, stop=True,
+            )
+            score_ps.append(bank)
+
+        v_codes = {}
+        v_scales = {}
+        turned = {}
+
+        def gather_and_turn(b, g):
+            picked = ring.tile([P, KP], F32, name="picked")
+            nc.vector.tensor_copy(picked[:], v_pool[b][:].indirect(offsets[:, g * COLS : (g + 1) * COLS]))
+            bank = psum_v.tile([P, PACK, P], F32, name="turned")
+            for t in range(PACK):
+                nc.tensor.transpose(bank[:, t, :], picked[:, t : KP : PACK], ident[:])
+            turned[b, g] = bank
+
+        woven = {}
+
+        def scale_values(b, g):
+            bank = turned[b, g]
+            v_bf = ring.tile([P, P, PACK], BF16, name="v_bf", align_bytes=64)
+            if (b, g) in ON_VECTOR:
+                nc.vector.tensor_tensor(
+                    v_bf[:], bank[:].rearrange("p t e -> p e t"),
+                    vsc_col[:, g : g + 1, :].to_broadcast([P, P, PACK]), ALU.mult,
+                )
+            else:
+                planes = ring.tile([P, PACK, P], BF16, name="planes")
+                for t in range(PACK):
+                    nc.scalar.activation(planes[:, t, :], bank[:, t, :], ACT.Copy, scale=vsc_col[:, g, t : t + 1])
+                nc.scalar.copy(v_bf[:], planes[:].rearrange("p t e -> p e t"))
+            woven[b, g] = v_bf
+
+        def quantize_values(b, g):
+            codes = keep.tile([P, P], U32, name="v_codes%d%d" % (b, g), align_bytes=64)
+            scales = keep.tile([P, P], U8, name="v_scales%d%d" % (b, g), align_bytes=64)
+            nc.vector.quantize_mx(out=codes[:].bitcast(FP8X4), scales=scales[:], in_=woven[b, g][:].rearrange("p e t -> p (e t)"))
+            v_codes[b, g] = codes
+            v_scales[b, g] = scales
+
+        gather_and_turn(0, 0)
+
+        s_sb = keep.tile([P, I], F32, name="s_sb")
+        for g in range(PASSES):
+            cols = slice(g * KP, (g + 1) * KP)
+            nc.vector.tensor_tensor(s_sb[:, cols], score_ps[g][:], mask_sb[:, cols], ALU.add)
+        neg_max = keep.tile([P, 1], F32, name="neg_max")
+        nc.vector.tensor_reduce(neg_max[:], s_sb[:], AX.X, ALU.max, negate=True)
+        p_sb = keep.tile([P, I], F32, name="p_sb")
+        row_sum = keep.tile([P, 1], F32, name="row_sum")
+        nc.scalar.activation(p_sb[:], s_sb[:], ACT.Exp, bias=neg_max[:], accum_out=row_sum[:])
+
+        scale_values(0, 0)
+        gather_and_turn(0, 1)
+        gather_and_turn(1, 0)
+        quantize_values(0, 0)
+        scale_values(0, 1)
+
+        inv_sum = keep.tile([P, 1], F32, name="inv_sum")
+        nc.vector.reciprocal(inv_sum[:], row_sum[:])
+        w_codes = []
+        w_scales = []
+        w_woven = []
+        for g in range(PASSES):
+            cols = slice(g * KP, (g + 1) * KP)
+            w_bf = keep.tile([P, KP], BF16, name="w_bf%d" % g, align_bytes=64)
+            nc.vector.scalar_tensor_tensor(
+                w_bf[:].rearrange("p (n t) -> p n t", t=PACK),
+                p_sb[:, cols].rearrange("p (n t) -> p n t", t=PACK),
+                inv_sum[:],
+                size_ps[g][:].rearrange("p t n -> p n t"),
+                ALU.mult, ALU.mult,
+            )
+            words = w_bf[:].bitcast(F32)
+            bank = psum.tile([P, 2, Q], F32, name="w_ps%d" % g, tag="early")
+            for u in range(2):
+                nc.tensor.transpose(bank[:, u, :], words[:, u : KP // 2 : 2], ident[:])
+            wt = keep.tile([P, Q, 2], F32, name="wt%d" % g, align_bytes=64)
+            nc.scalar.copy(wt[:], bank[:].rearrange("p u q -> p q u"))
+            w_woven.append(wt)
+
+        gather_and_turn(1, 1)
+        quantize_values(0, 1)
+        scale_values(1, 0)
+        for g in range(PASSES):
+            codes = keep.tile([P, Q], U32, name="w_codes%d" % g, align_bytes=64)
+            scales = keep.tile([P, Q], U8, name="w_scales%d" % g, align_bytes=64)
+            nc.vector.quantize_mx(
+                out=codes[:].bitcast(FP8X4), scales=scales[:],
+                in_=w_woven[g][:].rearrange("p q u -> p (q u)").bitcast(BF16),
+            )
+            w_codes.append(codes)
+            w_scales.append(scales)
+
+        units = [(b, g) for b in range(BLOCKS) for g in range(PASSES)]
+        for n in range(4, len(units) + 2):
+            if n < len(units):
+                gather_and_turn(*units[n])
+            if n - 1 < len(units):
+                scale_values(*units[n - 1])
+            quantize_values(*units[n - 2])
+
+        for first, last in ((0, 3), (3, 4)):
+            acc = psum.tile([P, (last - first) * P], F32, name="acc%d" % first, tag="late")
+            for b in range(first, last):
+                for g in range(PASSES):
+                    nc.tensor.matmul_mx(
+                        out=acc[:, (b - first) * P : (b - first + 1) * P],
+                        lhsT=w_codes[g][:].bitcast(FP8X4), lhsT_scale=w_scales[g][:],
+                        rhs=v_codes[b, g][:].bitcast(FP8X4), rhs_scale=v_scales[b, g][:],
+                        start=(g == 0), stop=(g == PASSES - 1),
+                    )
+            result = keep.tile([P, (last - first) * P], F32, name="result%d" % first)
+            nc.scalar.copy(result[:], acc[:])
+            nc.sync.dma_start(out[:, first * P : last * P], result[:])

@@ -23,7 +23,6 @@ KP = P * PACK
 PASSES = I // KP
 BLOCKS = E // P
 COLS = KP // 16
-ON_VECTOR = [(3, 1)]
 
 
 def tile_attend_beamcache_kernel(tc, query, keys_words, keys_scales, mask, size, vsc, vals, offs, out):
@@ -36,11 +35,15 @@ def tile_attend_beamcache_kernel(tc, query, keys_words, keys_scales, mask, size,
 
         offsets = keep.tile([P, I // 16], U16, name="offsets")
         nc.sync.dma_start(offsets[:], offs)
+        vsc_col = keep.tile([P, PASSES, PACK], F32, name="vsc_col")
+        nc.scalar.dma_start(vsc_col[:], vsc.rearrange("(g p t) o -> p g (t o)", g=PASSES, t=PACK))
+        size_col = keep.tile([P, PASSES, PACK], F32, name="size_col")
+        nc.scalar.dma_start(size_col[:], size.rearrange("o (g p t) -> p (o g) t", g=PASSES, t=PACK))
 
         ks_pool = keep.tile([P, T], U8, name="ks_pool", align_bytes=64)
-        nc.gpsimd.memset(ks_pool[:].bitcast(I32), 0)
+        nc.vector.memset(ks_pool[:].bitcast(I32), 0)
         for quad in range(4):
-            nc.scalar.dma_start(
+            nc.sync.dma_start(
                 ks_pool[32 * quad : 32 * quad + 4, :].bitcast(I32),
                 keys_scales[0, 4 * quad : 4 * quad + 4, :].bitcast(I32),
             )
@@ -55,17 +58,23 @@ def tile_attend_beamcache_kernel(tc, query, keys_words, keys_scales, mask, size,
         for b in range(1, BLOCKS):
             nc.sync.dma_start(v_pool[b][:], vals[b * P : (b + 1) * P, :])
 
-        size_col = keep.tile([P, PASSES, PACK], F32, name="size_col")
-        nc.scalar.dma_start(size_col[:], size.rearrange("o (g p t) -> p (o g) t", g=PASSES, t=PACK))
-        vsc_col = keep.tile([P, PASSES, PACK], F32, name="vsc_col")
-        nc.scalar.dma_start(vsc_col[:], vsc.rearrange("(g p t) o -> p g (t o)", g=PASSES, t=PACK))
         ident = keep.tile([P, P], F32, name="ident")
         make_identity(nc, ident[:])
 
-        ks = keep.tile([P, I], U8, name="ks", align_bytes=64)
-        nc.vector.tensor_copy(ks[:], ks_pool[:].indirect(offsets[:]))
         kw = keep.tile([P, I], U32, name="kw", align_bytes=64)
         nc.vector.tensor_copy(kw[:], kw_pool[:].bitcast(U32).indirect(offsets[:]))
+        ks = keep.tile([P, I], U8, name="ks", align_bytes=64)
+        nc.vector.tensor_copy(ks[:], ks_pool[:].indirect(offsets[:]))
+
+        vsc_row = keep.tile([P, I], F32, name="vsc_row")
+        for g in range(PASSES):
+            bank = psum_v.tile([P, PACK, P], F32, name="vsc_ps%d" % g, tag="turn")
+            for t in range(PACK):
+                nc.tensor.transpose(bank[:, t, :], vsc_col[:, g, t : t + 1].to_broadcast([P, P]), ident[:])
+            nc.scalar.copy(
+                vsc_row[:, g * KP : (g + 1) * KP].rearrange("p (n t) -> p n t", t=PACK),
+                bank[:].rearrange("p t n -> p n t"),
+            )
 
         q_bf = keep.tile([P, Q, PACK], BF16, name="q_bf", align_bytes=64)
         nc.scalar.copy(q_bf[:], q_raw[:].rearrange("p j q -> p q j"))
@@ -92,41 +101,39 @@ def tile_attend_beamcache_kernel(tc, query, keys_words, keys_scales, mask, size,
 
         v_codes = {}
         v_scales = {}
-        turned = {}
-
-        def gather_and_turn(b, g):
-            picked = ring.tile([P, KP], F32, name="picked")
-            nc.vector.tensor_copy(picked[:], v_pool[b][:].indirect(offsets[:, g * COLS : (g + 1) * COLS]))
-            bank = psum_v.tile([P, PACK, P], F32, name="turned")
-            for t in range(PACK):
-                nc.tensor.transpose(bank[:, t, :], picked[:, t : KP : PACK], ident[:])
-            turned[b, g] = bank
-
         woven = {}
 
-        def scale_values(b, g):
-            bank = turned[b, g]
-            v_bf = ring.tile([P, P, PACK], BF16, name="v_bf", align_bytes=64)
-            if (b, g) in ON_VECTOR:
-                nc.vector.tensor_tensor(
-                    v_bf[:], bank[:].rearrange("p t e -> p e t"),
-                    vsc_col[:, g : g + 1, :].to_broadcast([P, P, PACK]), ALU.mult,
-                )
-            else:
-                planes = ring.tile([P, PACK, P], BF16, name="planes")
-                for t in range(PACK):
-                    nc.scalar.activation(planes[:, t, :], bank[:, t, :], ACT.Copy, scale=vsc_col[:, g, t : t + 1])
-                nc.scalar.copy(v_bf[:], planes[:].rearrange("p t e -> p e t"))
-            woven[b, g] = v_bf
+        def gather_and_turn(b, first, last):
+            n = last - first
+            scaled = ring.tile([P, n * KP], F32, name="scaled")
+            nc.vector.tensor_tensor(
+                scaled[:], v_pool[b][:].indirect(offsets[:, first * COLS : last * COLS]),
+                vsc_row[:, first * KP : last * KP], ALU.mult,
+            )
+            v_words = ring.tile([P, n, P, 2], F32, name="v_words", align_bytes=64)
+            for k in range(n):
+                halves = ring.tile([P, 2, P, 2], BF16, name="halves")
+                nc.scalar.copy(halves[:], scaled[:, k * KP : (k + 1) * KP].rearrange("e (n u h) -> e u n h", u=2, h=2))
+                words = halves[:].rearrange("e u n h -> e (u n h)").bitcast(F32)
+                bank = psum_v.tile([P, 2, P], F32, name="turned", tag="turn")
+                for u in range(2):
+                    nc.tensor.transpose(bank[:, u, :], words[:, u * P : (u + 1) * P], ident[:])
+                nc.scalar.copy(v_words[:, k], bank[:].rearrange("p u e -> p e u"))
+            woven[b, first] = v_words
 
-        def quantize_values(b, g):
-            codes = keep.tile([P, P], U32, name="v_codes%d%d" % (b, g), align_bytes=64)
-            scales = keep.tile([P, P], U8, name="v_scales%d%d" % (b, g), align_bytes=64)
-            nc.vector.quantize_mx(out=codes[:].bitcast(FP8X4), scales=scales[:], in_=woven[b, g][:].rearrange("p e t -> p (e t)"))
-            v_codes[b, g] = codes
-            v_scales[b, g] = scales
+        def quantize_values(b, first, last):
+            n = last - first
+            codes = keep.tile([P, n * P], U32, name="v_codes%d%d" % (b, first), align_bytes=64)
+            scales = keep.tile([P, n * P], U8, name="v_scales%d%d" % (b, first), align_bytes=64)
+            nc.vector.quantize_mx(
+                out=codes[:].bitcast(FP8X4), scales=scales[:],
+                in_=woven[b, first][:].rearrange("p k e u -> p (k e u)").bitcast(BF16),
+            )
+            for k in range(n):
+                v_codes[b, first + k] = codes[:, k * P : (k + 1) * P]
+                v_scales[b, first + k] = scales[:, k * P : (k + 1) * P]
 
-        gather_and_turn(0, 0)
+        gather_and_turn(0, 0, 2)
 
         s_sb = keep.tile([P, I], F32, name="s_sb")
         for g in range(PASSES):
@@ -138,17 +145,12 @@ def tile_attend_beamcache_kernel(tc, query, keys_words, keys_scales, mask, size,
         row_sum = keep.tile([P, 1], F32, name="row_sum")
         nc.scalar.activation(p_sb[:], s_sb[:], ACT.Exp, bias=neg_max[:], accum_out=row_sum[:])
 
-        scale_values(0, 0)
-        gather_and_turn(0, 1)
-        gather_and_turn(1, 0)
-        quantize_values(0, 0)
-        scale_values(0, 1)
-
+        gather_and_turn(1, 0, 2)
         inv_sum = keep.tile([P, 1], F32, name="inv_sum")
         nc.vector.reciprocal(inv_sum[:], row_sum[:])
-        w_codes = []
-        w_scales = []
-        w_woven = []
+        quantize_values(0, 0, 2)
+
+        wt = keep.tile([P, PASSES, Q, 2], F32, name="wt", align_bytes=64)
         for g in range(PASSES):
             cols = slice(g * KP, (g + 1) * KP)
             w_bf = keep.tile([P, KP], BF16, name="w_bf%d" % g, align_bytes=64)
@@ -163,30 +165,24 @@ def tile_attend_beamcache_kernel(tc, query, keys_words, keys_scales, mask, size,
             bank = psum.tile([P, 2, Q], F32, name="w_ps%d" % g, tag="early")
             for u in range(2):
                 nc.tensor.transpose(bank[:, u, :], words[:, u : KP // 2 : 2], ident[:])
-            wt = keep.tile([P, Q, 2], F32, name="wt%d" % g, align_bytes=64)
-            nc.scalar.copy(wt[:], bank[:].rearrange("p u q -> p q u"))
-            w_woven.append(wt)
+            nc.scalar.copy(wt[:, g], bank[:].rearrange("p u q -> p q u"))
 
-        gather_and_turn(1, 1)
-        quantize_values(0, 1)
-        scale_values(1, 0)
-        for g in range(PASSES):
-            codes = keep.tile([P, Q], U32, name="w_codes%d" % g, align_bytes=64)
-            scales = keep.tile([P, Q], U8, name="w_scales%d" % g, align_bytes=64)
-            nc.vector.quantize_mx(
-                out=codes[:].bitcast(FP8X4), scales=scales[:],
-                in_=w_woven[g][:].rearrange("p q u -> p (q u)").bitcast(BF16),
-            )
-            w_codes.append(codes)
-            w_scales.append(scales)
+        gather_and_turn(2, 0, 2)
+        quantize_values(1, 0, 2)
+        w_all = keep.tile([P, PASSES * Q], U32, name="w_codes", align_bytes=64)
+        w_all_scales = keep.tile([P, PASSES * Q], U8, name="w_scales", align_bytes=64)
+        nc.vector.quantize_mx(
+            out=w_all[:].bitcast(FP8X4), scales=w_all_scales[:],
+            in_=wt[:].rearrange("p g q u -> p (g q u)").bitcast(BF16),
+        )
+        w_codes = [w_all[:, g * Q : (g + 1) * Q] for g in range(PASSES)]
+        w_scales = [w_all_scales[:, g * Q : (g + 1) * Q] for g in range(PASSES)]
 
-        units = [(b, g) for b in range(BLOCKS) for g in range(PASSES)]
-        for n in range(4, len(units) + 2):
-            if n < len(units):
-                gather_and_turn(*units[n])
-            if n - 1 < len(units):
-                scale_values(*units[n - 1])
-            quantize_values(*units[n - 2])
+        gather_and_turn(3, 0, 1)
+        gather_and_turn(3, 1, 2)
+        quantize_values(2, 0, 2)
+        quantize_values(3, 0, 1)
+        quantize_values(3, 1, 2)
 
         for first, last in ((0, 3), (3, 4)):
             acc = psum.tile([P, (last - first) * P], F32, name="acc%d" % first, tag="late")
@@ -194,8 +190,8 @@ def tile_attend_beamcache_kernel(tc, query, keys_words, keys_scales, mask, size,
                 for g in range(PASSES):
                     nc.tensor.matmul_mx(
                         out=acc[:, (b - first) * P : (b - first + 1) * P],
-                        lhsT=w_codes[g][:].bitcast(FP8X4), lhsT_scale=w_scales[g][:],
-                        rhs=v_codes[b, g][:].bitcast(FP8X4), rhs_scale=v_scales[b, g][:],
+                        lhsT=w_codes[g].bitcast(FP8X4), lhsT_scale=w_scales[g],
+                        rhs=v_codes[b, g].bitcast(FP8X4), rhs_scale=v_scales[b, g],
                         start=(g == 0), stop=(g == PASSES - 1),
                     )
             result = keep.tile([P, (last - first) * P], F32, name="result%d" % first)

@@ -29,9 +29,7 @@ def tile_attend_beamcache_kernel(tc, query, keys_words, keys_scales, mask, size,
     nc = tc.nc
     with ExitStack() as ctx:
         keep = ctx.enter_context(tc.tile_pool(name="keep", bufs=1))
-        ring = ctx.enter_context(tc.tile_pool(name="ring", bufs=3))
-        psum = ctx.enter_context(tc.psum_pool(name="psum", bufs=2))
-        psum_v = ctx.enter_context(tc.psum_pool(name="psum_v", bufs=4))
+        psum = ctx.enter_context(tc.psum_pool(name="psum", bufs=1))
 
         offsets = keep.tile([P, I // 16], U16, name="offsets")
         nc.sync.dma_start(offsets[:], offs)
@@ -63,12 +61,10 @@ def tile_attend_beamcache_kernel(tc, query, keys_words, keys_scales, mask, size,
 
         kw = keep.tile([P, I], U32, name="kw", align_bytes=64)
         nc.vector.tensor_copy(kw[:], kw_pool[:].bitcast(U32).indirect(offsets[:]))
-        ks = keep.tile([P, I], U8, name="ks", align_bytes=64)
-        nc.vector.tensor_copy(ks[:], ks_pool[:].indirect(offsets[:]))
 
-        vsc_row = keep.tile([P, I], F32, name="vsc_row")
+        vsc_row = keep.tile([P, I], F32, name="vsc_row", tag="reused", align_bytes=64)
         for g in range(PASSES):
-            bank = psum_v.tile([P, PACK, P], F32, name="vsc_ps%d" % g, tag="turn")
+            bank = psum.tile([P, PACK, P], F32, name="vsc_ps%d" % g, tag="bank%d" % (4 + g))
             for t in range(PACK):
                 nc.tensor.transpose(bank[:, t, :], vsc_col[:, g, t : t + 1].to_broadcast([P, P]), ident[:])
             nc.scalar.copy(
@@ -78,13 +74,17 @@ def tile_attend_beamcache_kernel(tc, query, keys_words, keys_scales, mask, size,
 
         q_bf = keep.tile([P, Q, PACK], BF16, name="q_bf", align_bytes=64)
         nc.scalar.copy(q_bf[:], q_raw[:].rearrange("p j q -> p q j"))
-        q_codes = keep.tile([P, Q], U32, name="q_codes", align_bytes=64)
+        q_codes = keep.tile([P, Q], U32, name="q_codes", tag="q_codes", align_bytes=64)
         q_scales = keep.tile([P, Q], U8, name="q_scales", align_bytes=64)
         nc.vector.quantize_mx(out=q_codes[:].bitcast(FP8X4), scales=q_scales[:], in_=q_bf[:].rearrange("p q j -> p (q j)"))
 
+        ks = keep.tile([P, I], U8, name="ks", align_bytes=64)
+        for g in range(PASSES):
+            nc.vector.tensor_copy(ks[:, g * KP : (g + 1) * KP], ks_pool[:].indirect(offsets[:, g * COLS : (g + 1) * COLS]))
+
         size_ps = []
         for g in range(PASSES):
-            bank = psum.tile([P, PACK, P], F32, name="size_ps%d" % g, tag="late")
+            bank = psum.tile([P, PACK, P], F32, name="size_ps%d" % g, tag="bank%d" % g)
             for t in range(PACK):
                 nc.tensor.transpose(bank[:, t, :], size_col[:, g, t : t + 1].to_broadcast([P, P]), ident[:])
             size_ps.append(bank)
@@ -92,7 +92,7 @@ def tile_attend_beamcache_kernel(tc, query, keys_words, keys_scales, mask, size,
         score_ps = []
         for g in range(PASSES):
             cols = slice(g * KP, (g + 1) * KP)
-            bank = psum.tile([P, KP], F32, name="score_ps%d" % g, tag="early")
+            bank = psum.tile([P, KP], F32, name="score_ps%d" % g, tag="bank%d" % (2 + g))
             nc.tensor.matmul_mx(
                 out=bank[:], lhsT=q_codes[:].bitcast(FP8X4), lhsT_scale=q_scales[:],
                 rhs=kw[:, cols].bitcast(FP8X4), rhs_scale=ks[:, cols], start=True, stop=True,
@@ -102,58 +102,74 @@ def tile_attend_beamcache_kernel(tc, query, keys_words, keys_scales, mask, size,
         v_codes = {}
         v_scales = {}
         woven = {}
+        halves = {}
 
-        def gather_and_turn(b, first, last):
-            n = last - first
-            scaled = ring.tile([P, n * KP], F32, name="scaled")
+        def gather(b, lo, hi, tag=None):
+            name = "scaled%d_%d" % (b, lo)
+            scaled = keep.tile([P, hi - lo], F32, name=name, tag=tag or name, align_bytes=64)
             nc.vector.tensor_tensor(
-                scaled[:], v_pool[b][:].indirect(offsets[:, first * COLS : last * COLS]),
-                vsc_row[:, first * KP : last * KP], ALU.mult,
+                scaled[:], v_pool[b][:].indirect(offsets[:, lo // 16 : hi // 16]), vsc_row[:, lo:hi], ALU.mult
             )
-            v_words = ring.tile([P, n, P, 2], F32, name="v_words", align_bytes=64)
-            for k in range(n):
-                halves = ring.tile([P, 2, P, 2], BF16, name="halves")
-                nc.scalar.copy(halves[:], scaled[:, k * KP : (k + 1) * KP].rearrange("e (n u h) -> e u n h", u=2, h=2))
-                words = halves[:].rearrange("e u n h -> e (u n h)").bitcast(F32)
-                bank = psum_v.tile([P, 2, P], F32, name="turned", tag="turn")
-                for u in range(2):
-                    nc.tensor.transpose(bank[:, u, :], words[:, u * P : (u + 1) * P], ident[:])
-                nc.scalar.copy(v_words[:, k], bank[:].rearrange("p u e -> p e u"))
-            woven[b, first] = v_words
+            return scaled
 
-        def quantize_values(b, first, last):
+        def cast(b, lo, hi, scaled, copy):
+            g = lo // KP
+            if (b, g) not in halves:
+                halves[b, g] = keep.tile([P, 2, P, 2], BF16, name="halves%d%d" % (b, g), align_bytes=64)
+            copy(
+                halves[b, g][:, :, (lo - g * KP) // PACK : (hi - g * KP) // PACK, :],
+                scaled.rearrange("e (n u h) -> e u n h", u=2, h=2),
+            )
+
+        def turn(b, g, bank_tag, v_words):
+            words = halves[b, g][:].rearrange("e u n h -> e (u n h)").bitcast(F32)
+            bank = psum.tile([P, 2, P], F32, name="turned%d%d" % (b, g), tag=bank_tag)
+            for u in range(2):
+                nc.tensor.transpose(bank[:, u, :], words[:, u * P : (u + 1) * P], ident[:])
+            nc.scalar.copy(v_words, bank[:].rearrange("p u e -> p e u"))
+
+        def block(b, banks, tags):
+            v_words = keep.tile([P, PASSES, P, 2], F32, name="v_words%d" % b, align_bytes=64)
+            width = I // len(tags)
+            pieces = [gather(b, k * width, (k + 1) * width, tag) for k, tag in enumerate(tags)]
+            for g in range(PASSES):
+                k, at = divmod(g * KP, width)
+                cast(b, g * KP, (g + 1) * KP, pieces[k][:, at : at + KP], nc.scalar.copy)
+            for g in range(PASSES):
+                turn(b, g, banks[g], v_words[:, g])
+            woven[b, 0] = v_words
+
+        def quantize_values(b, first, last, codes):
             n = last - first
-            codes = keep.tile([P, n * P], U32, name="v_codes%d%d" % (b, first), align_bytes=64)
             scales = keep.tile([P, n * P], U8, name="v_scales%d%d" % (b, first), align_bytes=64)
             nc.vector.quantize_mx(
-                out=codes[:].bitcast(FP8X4), scales=scales[:],
+                out=codes.bitcast(FP8X4), scales=scales[:],
                 in_=woven[b, first][:].rearrange("p k e u -> p (k e u)").bitcast(BF16),
             )
             for k in range(n):
                 v_codes[b, first + k] = codes[:, k * P : (k + 1) * P]
                 v_scales[b, first + k] = scales[:, k * P : (k + 1) * P]
 
-        gather_and_turn(0, 0, 2)
+        block(0, ("bank6", "bank7"), [None])
 
-        s_sb = keep.tile([P, I], F32, name="s_sb")
+        s_sb = keep.tile([P, I], F32, name="s_sb", tag="s_sb", align_bytes=64)
         for g in range(PASSES):
             cols = slice(g * KP, (g + 1) * KP)
             nc.vector.tensor_tensor(s_sb[:, cols], score_ps[g][:], mask_sb[:, cols], ALU.add)
         neg_max = keep.tile([P, 1], F32, name="neg_max")
         nc.vector.tensor_reduce(neg_max[:], s_sb[:], AX.X, ALU.max, negate=True)
-        p_sb = keep.tile([P, I], F32, name="p_sb")
-        row_sum = keep.tile([P, 1], F32, name="row_sum")
+        p_sb = keep.tile([P, I], F32, name="p_sb", tag="p_sb", align_bytes=64)
+        row_sum = keep.tile([P, 1], F32, name="row_sum", tag="row_sum", align_bytes=64)
         nc.scalar.activation(p_sb[:], s_sb[:], ACT.Exp, bias=neg_max[:], accum_out=row_sum[:])
 
-        gather_and_turn(1, 0, 2)
-        inv_sum = keep.tile([P, 1], F32, name="inv_sum")
+        block(1, ("bank4", "bank5"), [None])
+        inv_sum = keep.tile([P, 1], F32, name="inv_sum", tag="inv_sum", align_bytes=64)
         nc.vector.reciprocal(inv_sum[:], row_sum[:])
-        quantize_values(0, 0, 2)
 
-        wt = keep.tile([P, PASSES, Q, 2], F32, name="wt", align_bytes=64)
+        wt = keep.tile([P, PASSES, Q, 2], F32, name="wt", tag="wt", align_bytes=64)
         for g in range(PASSES):
             cols = slice(g * KP, (g + 1) * KP)
-            w_bf = keep.tile([P, KP], BF16, name="w_bf%d" % g, align_bytes=64)
+            w_bf = keep.tile([P, KP], BF16, name="w_bf%d" % g, tag="w_bf%d" % g, align_bytes=64)
             nc.vector.scalar_tensor_tensor(
                 w_bf[:].rearrange("p (n t) -> p n t", t=PACK),
                 p_sb[:, cols].rearrange("p (n t) -> p n t", t=PACK),
@@ -162,13 +178,12 @@ def tile_attend_beamcache_kernel(tc, query, keys_words, keys_scales, mask, size,
                 ALU.mult, ALU.mult,
             )
             words = w_bf[:].bitcast(F32)
-            bank = psum.tile([P, 2, Q], F32, name="w_ps%d" % g, tag="early")
+            bank = psum.tile([P, 2, Q], F32, name="w_ps%d" % g, tag="bank%d" % (2 + g))
             for u in range(2):
                 nc.tensor.transpose(bank[:, u, :], words[:, u : KP // 2 : 2], ident[:])
             nc.scalar.copy(wt[:, g], bank[:].rearrange("p u q -> p q u"))
 
-        gather_and_turn(2, 0, 2)
-        quantize_values(1, 0, 2)
+        block(2, ("bank6", "bank7"), ["row_sum", "inv_sum"])
         w_all = keep.tile([P, PASSES * Q], U32, name="w_codes", align_bytes=64)
         w_all_scales = keep.tile([P, PASSES * Q], U8, name="w_scales", align_bytes=64)
         nc.vector.quantize_mx(
@@ -178,14 +193,24 @@ def tile_attend_beamcache_kernel(tc, query, keys_words, keys_scales, mask, size,
         w_codes = [w_all[:, g * Q : (g + 1) * Q] for g in range(PASSES)]
         w_scales = [w_all_scales[:, g * Q : (g + 1) * Q] for g in range(PASSES)]
 
-        gather_and_turn(3, 0, 1)
-        gather_and_turn(3, 1, 2)
-        quantize_values(2, 0, 2)
-        quantize_values(3, 0, 1)
-        quantize_values(3, 1, 2)
+        last = BLOCKS - 1
+        for g in range(PASSES):
+            woven[last, g] = keep.tile([P, 1, P, 2], F32, name="v_words%d%d" % (last, g), align_bytes=64)
+        cast(last, 0, KP, gather(last, 0, KP, "w_bf0")[:], nc.scalar.copy)
+        cast(last, KP, I - P, gather(last, KP, I - P, "w_bf1")[:], nc.scalar.copy)
+        turn(last, 0, "bank4", woven[last, 0][:, 0])
+        cast(last, I - P, I, gather(last, I - P, I, "w_bf0")[:], nc.vector.tensor_copy)
+        turn(last, 1, "bank5", woven[last, 1][:, 0])
+        late_codes = keep.tile([P, 8 * P], U32, name="late_codes", tag="reused", align_bytes=64)
+        for b in range(last):
+            quantize_values(b, 0, 2, late_codes[:, 2 * b * P : 2 * (b + 1) * P])
+        quantize_values(3, 0, 1, late_codes[:, 6 * P : 7 * P])
+        quantize_values(3, 1, 2, late_codes[:, 7 * P : 8 * P])
 
-        for first, last in ((0, 3), (3, 4)):
-            acc = psum.tile([P, (last - first) * P], F32, name="acc%d" % first, tag="late")
+        for first, last, tag, copy in (
+            (0, 3, "bank4", nc.scalar.copy), (3, 4, "bank1", nc.vector.tensor_copy)
+        ):
+            acc = psum.tile([P, (last - first) * P], F32, name="acc%d" % first, tag=tag)
             for b in range(first, last):
                 for g in range(PASSES):
                     nc.tensor.matmul_mx(
@@ -195,5 +220,5 @@ def tile_attend_beamcache_kernel(tc, query, keys_words, keys_scales, mask, size,
                         start=(g == 0), stop=(g == PASSES - 1),
                     )
             result = keep.tile([P, (last - first) * P], F32, name="result%d" % first)
-            nc.scalar.copy(result[:], acc[:])
+            copy(result[:], acc[:])
             nc.sync.dma_start(out[:, first * P : last * P], result[:])

@@ -23,6 +23,7 @@ KP = P * PACK
 PASSES = I // KP
 BLOCKS = E // P
 COLS = KP // 16
+CHUNKS = I // P
 
 
 def tile_attend_beamcache_kernel(tc, query, keys_words, keys_scales, mask, size, vsc, vals, offs, out):
@@ -33,11 +34,12 @@ def tile_attend_beamcache_kernel(tc, query, keys_words, keys_scales, mask, size,
 
         offsets = keep.tile([P, I // 16], U16, name="offsets")
         nc.sync.dma_start(offsets[:], offs)
-        vsc_col = keep.tile([P, PASSES, PACK], F32, name="vsc_col")
-        nc.scalar.dma_start(vsc_col[:], vsc.rearrange("(g p t) o -> p g (t o)", g=PASSES, t=PACK))
-        size_col = keep.tile([P, PASSES, PACK], F32, name="size_col")
-        nc.scalar.dma_start(size_col[:], size.rearrange("o (g p t) -> p (o g) t", g=PASSES, t=PACK))
-
+        vsc_col = keep.tile([P, CHUNKS], F32, name="vsc_col")
+        nc.sync.dma_start(vsc_col[:], vsc.rearrange("(p c) o -> p (c o)", c=CHUNKS))
+        size_col = keep.tile([P, PASSES, 2 * PACK], F32, name="size_col")
+        nc.sync.dma_start(size_col[:, :, 0:PACK], size.rearrange("o (g p t) -> p (o g) t", g=PASSES, t=PACK))
+        kw_pool = keep.tile([P, T], I32, name="kw_pool", align_bytes=64)
+        nc.sync.dma_start(kw_pool[:], keys_words[0].rearrange("p n t -> p (n t)").bitcast(I32))
         ks_pool = keep.tile([P, T], U8, name="ks_pool", align_bytes=64)
         nc.vector.memset(ks_pool[:].bitcast(I32), 0)
         for quad in range(4):
@@ -45,8 +47,6 @@ def tile_attend_beamcache_kernel(tc, query, keys_words, keys_scales, mask, size,
                 ks_pool[32 * quad : 32 * quad + 4, :].bitcast(I32),
                 keys_scales[0, 4 * quad : 4 * quad + 4, :].bitcast(I32),
             )
-        kw_pool = keep.tile([P, T], I32, name="kw_pool", align_bytes=64)
-        nc.sync.dma_start(kw_pool[:], keys_words[0].rearrange("p n t -> p (n t)").bitcast(I32))
         q_raw = keep.tile([P, PACK, Q], F32, name="q_raw")
         nc.sync.dma_start(q_raw[:], query.rearrange("(p j) q -> p j q", j=PACK))
         v_pool = [keep.tile([P, T], F32, name="v_pool%d" % b, align_bytes=64) for b in range(BLOCKS)]
@@ -66,9 +66,9 @@ def tile_attend_beamcache_kernel(tc, query, keys_words, keys_scales, mask, size,
         for g in range(PASSES):
             bank = psum.tile([P, PACK, P], F32, name="vsc_ps%d" % g, tag="bank%d" % (4 + g))
             for t in range(PACK):
-                nc.tensor.transpose(bank[:, t, :], vsc_col[:, g, t : t + 1].to_broadcast([P, P]), ident[:])
+                nc.tensor.transpose(bank[:, t, :], vsc_col[:, g * PACK + t : g * PACK + t + 1].to_broadcast([P, P]), ident[:])
             nc.scalar.copy(
-                vsc_row[:, g * KP : (g + 1) * KP].rearrange("p (n t) -> p n t", t=PACK),
+                vsc_row[:].rearrange("p (n c) -> p n c", c=CHUNKS)[:, :, g * PACK : (g + 1) * PACK],
                 bank[:].rearrange("p t n -> p n t"),
             )
 
@@ -194,12 +194,12 @@ def tile_attend_beamcache_kernel(tc, query, keys_words, keys_scales, mask, size,
         w_scales = [w_all_scales[:, g * Q : (g + 1) * Q] for g in range(PASSES)]
 
         last = BLOCKS - 1
-        for g in range(PASSES):
-            woven[last, g] = keep.tile([P, 1, P, 2], F32, name="v_words%d%d" % (last, g), align_bytes=64)
         cast(last, 0, KP, gather(last, 0, KP, "w_bf0")[:], nc.scalar.copy)
         cast(last, KP, I - P, gather(last, KP, I - P, "w_bf1")[:], nc.scalar.copy)
+        woven[last, 0] = keep.tile([P, 1, P, 2], F32, name="v_words30", align_bytes=64)
+        woven[last, 1] = keep.tile([P, 1, P, 2], F32, name="v_words31", align_bytes=64)
         turn(last, 0, "bank4", woven[last, 0][:, 0])
-        cast(last, I - P, I, gather(last, I - P, I, "w_bf0")[:], nc.vector.tensor_copy)
+        cast(last, I - P, I, gather(last, I - P, I, "wt")[:], nc.vector.tensor_copy)
         turn(last, 1, "bank5", woven[last, 1][:, 0])
         late_codes = keep.tile([P, 8 * P], U32, name="late_codes", tag="reused", align_bytes=64)
         for b in range(last):

@@ -35,18 +35,15 @@ def tile_attend_beamcache_kernel(tc, query, keys_words, keys_scales, mask, size,
         offsets = keep.tile([P, I // 16], U16, name="offsets")
         nc.sync.dma_start(offsets[:], offs)
         vsc_col = keep.tile([P, CHUNKS], F32, name="vsc_col")
-        nc.sync.dma_start(vsc_col[:], vsc.rearrange("(p c) o -> p (c o)", c=CHUNKS))
+        nc.scalar.dma_start(vsc_col[:], vsc.rearrange("(p c) o -> p (c o)", c=CHUNKS))
         size_col = keep.tile([P, PASSES, 2 * PACK], F32, name="size_col")
-        nc.sync.dma_start(size_col[:, :, 0:PACK], size.rearrange("o (g p t) -> p (o g) t", g=PASSES, t=PACK))
+        nc.scalar.dma_start(size_col[:, :, 0:PACK], size.rearrange("o (g p t) -> p (o g) t", g=PASSES, t=PACK))
         kw_pool = keep.tile([P, T], I32, name="kw_pool", align_bytes=64)
         nc.sync.dma_start(kw_pool[:], keys_words[0].rearrange("p n t -> p (n t)").bitcast(I32))
         ks_pool = keep.tile([P, T], U8, name="ks_pool", align_bytes=64)
         nc.vector.memset(ks_pool[:].bitcast(I32), 0)
-        for quad in range(4):
-            nc.sync.dma_start(
-                ks_pool[32 * quad : 32 * quad + 4, :].bitcast(I32),
-                keys_scales[0, 4 * quad : 4 * quad + 4, :].bitcast(I32),
-            )
+        for r in range(4):
+            nc.sync.dma_start(ks_pool[r:P:32, :].bitcast(I32), keys_scales[0, r:16:4, :].bitcast(I32))
         q_raw = keep.tile([P, PACK, Q], F32, name="q_raw")
         nc.sync.dma_start(q_raw[:], query.rearrange("(p j) q -> p j q", j=PACK))
         v_pool = [keep.tile([P, T], F32, name="v_pool%d" % b, align_bytes=64) for b in range(BLOCKS)]
@@ -79,8 +76,7 @@ def tile_attend_beamcache_kernel(tc, query, keys_words, keys_scales, mask, size,
         nc.vector.quantize_mx(out=q_codes[:].bitcast(FP8X4), scales=q_scales[:], in_=q_bf[:].rearrange("p q j -> p (q j)"))
 
         ks = keep.tile([P, I], U8, name="ks", align_bytes=64)
-        for g in range(PASSES):
-            nc.vector.tensor_copy(ks[:, g * KP : (g + 1) * KP], ks_pool[:].indirect(offsets[:, g * COLS : (g + 1) * COLS]))
+        nc.vector.tensor_copy(ks[:], ks_pool[:].indirect(offsets[:]))
 
         size_ps = []
         for g in range(PASSES):
@@ -128,13 +124,11 @@ def tile_attend_beamcache_kernel(tc, query, keys_words, keys_scales, mask, size,
                 nc.tensor.transpose(bank[:, u, :], words[:, u * P : (u + 1) * P], ident[:])
             nc.scalar.copy(v_words, bank[:].rearrange("p u e -> p e u"))
 
-        def block(b, banks, tags):
+        def block(b, banks):
             v_words = keep.tile([P, PASSES, P, 2], F32, name="v_words%d" % b, align_bytes=64)
-            width = I // len(tags)
-            pieces = [gather(b, k * width, (k + 1) * width, tag) for k, tag in enumerate(tags)]
+            scaled = gather(b, 0, I)
             for g in range(PASSES):
-                k, at = divmod(g * KP, width)
-                cast(b, g * KP, (g + 1) * KP, pieces[k][:, at : at + KP], nc.scalar.copy)
+                cast(b, g * KP, (g + 1) * KP, scaled[:, g * KP : (g + 1) * KP], nc.scalar.copy)
             for g in range(PASSES):
                 turn(b, g, banks[g], v_words[:, g])
             woven[b, 0] = v_words
@@ -150,7 +144,7 @@ def tile_attend_beamcache_kernel(tc, query, keys_words, keys_scales, mask, size,
                 v_codes[b, first + k] = codes[:, k * P : (k + 1) * P]
                 v_scales[b, first + k] = scales[:, k * P : (k + 1) * P]
 
-        block(0, ("bank6", "bank7"), [None])
+        block(0, ("bank6", "bank7"))
 
         s_sb = keep.tile([P, I], F32, name="s_sb", tag="s_sb", align_bytes=64)
         for g in range(PASSES):
@@ -162,9 +156,11 @@ def tile_attend_beamcache_kernel(tc, query, keys_words, keys_scales, mask, size,
         row_sum = keep.tile([P, 1], F32, name="row_sum", tag="row_sum", align_bytes=64)
         nc.scalar.activation(p_sb[:], s_sb[:], ACT.Exp, bias=neg_max[:], accum_out=row_sum[:])
 
-        block(1, ("bank4", "bank5"), [None])
+        block(1, ("bank4", "bank5"))
         inv_sum = keep.tile([P, 1], F32, name="inv_sum", tag="inv_sum", align_bytes=64)
         nc.vector.reciprocal(inv_sum[:], row_sum[:])
+        woven[2, 0] = keep.tile([P, PASSES, P, 2], F32, name="v_words2", align_bytes=64)
+        early = gather(2, 0, KP, "s_sb")
 
         wt = keep.tile([P, PASSES, Q, 2], F32, name="wt", tag="wt", align_bytes=64)
         for g in range(PASSES):
@@ -183,7 +179,12 @@ def tile_attend_beamcache_kernel(tc, query, keys_words, keys_scales, mask, size,
                 nc.tensor.transpose(bank[:, u, :], words[:, u : KP // 2 : 2], ident[:])
             nc.scalar.copy(wt[:, g], bank[:].rearrange("p u q -> p q u"))
 
-        block(2, ("bank6", "bank7"), ["row_sum", "inv_sum"])
+        cast(2, 0, KP, early[:], nc.scalar.copy)
+        turn(2, 0, "bank6", woven[2, 0][:, 0])
+        cast(2, KP, I, gather(2, KP, I, "row_sum")[:], nc.scalar.copy)
+        turn(2, 1, "bank7", woven[2, 0][:, 1])
+        last = BLOCKS - 1
+        cast(last, 0, KP, gather(last, 0, KP, "w_bf0")[:], nc.scalar.copy)
         w_all = keep.tile([P, PASSES * Q], U32, name="w_codes", align_bytes=64)
         w_all_scales = keep.tile([P, PASSES * Q], U8, name="w_scales", align_bytes=64)
         nc.vector.quantize_mx(
@@ -193,8 +194,6 @@ def tile_attend_beamcache_kernel(tc, query, keys_words, keys_scales, mask, size,
         w_codes = [w_all[:, g * Q : (g + 1) * Q] for g in range(PASSES)]
         w_scales = [w_all_scales[:, g * Q : (g + 1) * Q] for g in range(PASSES)]
 
-        last = BLOCKS - 1
-        cast(last, 0, KP, gather(last, 0, KP, "w_bf0")[:], nc.scalar.copy)
         cast(last, KP, I - P, gather(last, KP, I - P, "w_bf1")[:], nc.scalar.copy)
         woven[last, 0] = keep.tile([P, 1, P, 2], F32, name="v_words30", align_bytes=64)
         woven[last, 1] = keep.tile([P, 1, P, 2], F32, name="v_words31", align_bytes=64)

@@ -22,8 +22,11 @@ PACK = 4
 KP = P * PACK
 PASSES = I // KP
 BLOCKS = E // P
-COLS = KP // 16
-CHUNKS = I // P
+LAST = BLOCKS - 1
+STRIPE = 16
+QUADRANT = 32
+PER_ROW = I // P
+CUT = I - 2 * P
 
 
 def tile_attend_beamcache_kernel(tc, query, keys_words, keys_scales, mask, size, vsc, vals, offs, out):
@@ -32,20 +35,22 @@ def tile_attend_beamcache_kernel(tc, query, keys_words, keys_scales, mask, size,
         keep = ctx.enter_context(tc.tile_pool(name="keep", bufs=1))
         psum = ctx.enter_context(tc.psum_pool(name="psum", bufs=1))
 
-        offsets = keep.tile([P, I // 16], U16, name="offsets")
+        offsets = keep.tile([P, I // STRIPE], U16, name="offsets")
         nc.sync.dma_start(offsets[:], offs)
-        vsc_col = keep.tile([P, CHUNKS], F32, name="vsc_col")
-        nc.scalar.dma_start(vsc_col[:], vsc.rearrange("(p c) o -> p (c o)", c=CHUNKS))
+        vsc_col = keep.tile([P, PER_ROW], F32, name="vsc_col")
+        nc.scalar.dma_start(vsc_col[:], vsc.rearrange("(n c) o -> n (c o)", c=PER_ROW))
         size_col = keep.tile([P, PASSES, 2 * PACK], F32, name="size_col")
         nc.scalar.dma_start(size_col[:, :, 0:PACK], size.rearrange("o (g p t) -> p (o g) t", g=PASSES, t=PACK))
         kw_pool = keep.tile([P, T], I32, name="kw_pool", align_bytes=64)
         nc.sync.dma_start(kw_pool[:], keys_words[0].rearrange("p n t -> p (n t)").bitcast(I32))
         ks_pool = keep.tile([P, T], U8, name="ks_pool", align_bytes=64)
         nc.vector.memset(ks_pool[:].bitcast(I32), 0)
-        for r in range(4):
-            nc.sync.dma_start(ks_pool[r:P:32, :].bitcast(I32), keys_scales[0, r:16:4, :].bitcast(I32))
+        for r in range(PACK):
+            nc.sync.dma_start(
+                ks_pool[r:P:QUADRANT, :].bitcast(I32), keys_scales[0, r : KP // QUADRANT : PACK, :].bitcast(I32)
+            )
         q_raw = keep.tile([P, PACK, Q], F32, name="q_raw")
-        nc.sync.dma_start(q_raw[:], query.rearrange("(p j) q -> p j q", j=PACK))
+        nc.sync.dma_start(q_raw[:], query.rearrange("(p t) q -> p t q", t=PACK))
         v_pool = [keep.tile([P, T], F32, name="v_pool%d" % b, align_bytes=64) for b in range(BLOCKS)]
         nc.sync.dma_start(v_pool[0][:], vals[0:P, :])
         mask_sb = keep.tile([P, I], F32, name="mask_sb")
@@ -59,21 +64,24 @@ def tile_attend_beamcache_kernel(tc, query, keys_words, keys_scales, mask, size,
         kw = keep.tile([P, I], U32, name="kw", align_bytes=64)
         nc.vector.tensor_copy(kw[:], kw_pool[:].bitcast(U32).indirect(offsets[:]))
 
-        vsc_row = keep.tile([P, I], F32, name="vsc_row", tag="reused", align_bytes=64)
-        for g in range(PASSES):
-            bank = psum.tile([P, PACK, P], F32, name="vsc_ps%d" % g, tag="bank%d" % (4 + g))
-            for t in range(PACK):
-                nc.tensor.transpose(bank[:, t, :], vsc_col[:, g * PACK + t : g * PACK + t + 1].to_broadcast([P, P]), ident[:])
+        vsc_row = keep.tile([P, I], F32, name="vsc_row", tag="vsc_row", align_bytes=64)
+        for half in range(PER_ROW // PACK):
+            bank = psum.tile([P, PACK, P], F32, name="vsc_ps%d" % half, tag="bank%d" % (4 + half))
+            for c in range(PACK):
+                column = half * PACK + c
+                nc.tensor.transpose(bank[:, c, :], vsc_col[:, column : column + 1].to_broadcast([P, P]), ident[:])
             nc.scalar.copy(
-                vsc_row[:].rearrange("p (n c) -> p n c", c=CHUNKS)[:, :, g * PACK : (g + 1) * PACK],
-                bank[:].rearrange("p t n -> p n t"),
+                vsc_row[:].rearrange("p (n c) -> p n c", c=PER_ROW)[:, :, half * PACK : (half + 1) * PACK],
+                bank[:].rearrange("p c n -> p n c"),
             )
 
         q_bf = keep.tile([P, Q, PACK], BF16, name="q_bf", align_bytes=64)
-        nc.scalar.copy(q_bf[:], q_raw[:].rearrange("p j q -> p q j"))
-        q_codes = keep.tile([P, Q], U32, name="q_codes", tag="q_codes", align_bytes=64)
+        nc.scalar.copy(q_bf[:], q_raw[:].rearrange("p t q -> p q t"))
+        q_codes = keep.tile([P, Q], U32, name="q_codes", align_bytes=64)
         q_scales = keep.tile([P, Q], U8, name="q_scales", align_bytes=64)
-        nc.vector.quantize_mx(out=q_codes[:].bitcast(FP8X4), scales=q_scales[:], in_=q_bf[:].rearrange("p q j -> p (q j)"))
+        nc.vector.quantize_mx(
+            out=q_codes[:].bitcast(FP8X4), scales=q_scales[:], in_=q_bf[:].rearrange("p q t -> p (q t)")
+        )
 
         ks = keep.tile([P, I], U8, name="ks", align_bytes=64)
         nc.vector.tensor_copy(ks[:], ks_pool[:].indirect(offsets[:]))
@@ -95,56 +103,50 @@ def tile_attend_beamcache_kernel(tc, query, keys_words, keys_scales, mask, size,
             )
             score_ps.append(bank)
 
+        pairs = {}
         v_codes = {}
         v_scales = {}
-        woven = {}
-        halves = {}
 
-        def gather(b, lo, hi, tag=None):
-            name = "scaled%d_%d" % (b, lo)
-            scaled = keep.tile([P, hi - lo], F32, name=name, tag=tag or name, align_bytes=64)
+        def gather(b, lo, hi, tag):
+            scaled = keep.tile([P, hi - lo], F32, name="scaled%d_%d" % (b, lo), tag=tag, align_bytes=64)
             nc.vector.tensor_tensor(
-                scaled[:], v_pool[b][:].indirect(offsets[:, lo // 16 : hi // 16]), vsc_row[:, lo:hi], ALU.mult
+                scaled[:], v_pool[b][:].indirect(offsets[:, lo // STRIPE : hi // STRIPE]), vsc_row[:, lo:hi], ALU.mult
             )
             return scaled
 
-        def cast(b, lo, hi, scaled, copy):
+        def round_to_pairs(b, lo, hi, scaled, copy):
             g = lo // KP
-            if (b, g) not in halves:
-                halves[b, g] = keep.tile([P, 2, P, 2], BF16, name="halves%d%d" % (b, g), align_bytes=64)
+            if (b, g) not in pairs:
+                pairs[b, g] = keep.tile([P, 2, P, 2], BF16, name="pairs%d%d" % (b, g), align_bytes=64)
             copy(
-                halves[b, g][:, :, (lo - g * KP) // PACK : (hi - g * KP) // PACK, :],
+                pairs[b, g][:, :, (lo - g * KP) // PACK : (hi - g * KP) // PACK, :],
                 scaled.rearrange("e (n u h) -> e u n h", u=2, h=2),
             )
 
-        def turn(b, g, bank_tag, v_words):
-            words = halves[b, g][:].rearrange("e u n h -> e (u n h)").bitcast(F32)
+        def turn_pairs(b, g, bank_tag, woven):
+            words = pairs[b, g][:].rearrange("e u n h -> e (u n h)").bitcast(F32)
             bank = psum.tile([P, 2, P], F32, name="turned%d%d" % (b, g), tag=bank_tag)
             for u in range(2):
                 nc.tensor.transpose(bank[:, u, :], words[:, u * P : (u + 1) * P], ident[:])
-            nc.scalar.copy(v_words, bank[:].rearrange("p u e -> p e u"))
+            nc.scalar.copy(woven, bank[:].rearrange("p u e -> p e u"))
 
-        def block(b, banks):
-            v_words = keep.tile([P, PASSES, P, 2], F32, name="v_words%d" % b, align_bytes=64)
-            scaled = gather(b, 0, I)
-            for g in range(PASSES):
-                cast(b, g * KP, (g + 1) * KP, scaled[:, g * KP : (g + 1) * KP], nc.scalar.copy)
-            for g in range(PASSES):
-                turn(b, g, banks[g], v_words[:, g])
-            woven[b, 0] = v_words
-
-        def quantize_values(b, first, last, codes):
-            n = last - first
-            scales = keep.tile([P, n * P], U8, name="v_scales%d%d" % (b, first), align_bytes=64)
+        def quantize_values(b, first, woven, codes):
+            count = woven.shape[1]
+            scales = keep.tile([P, count * P], U8, name="v_scales%d%d" % (b, first), align_bytes=64)
             nc.vector.quantize_mx(
                 out=codes.bitcast(FP8X4), scales=scales[:],
-                in_=woven[b, first][:].rearrange("p k e u -> p (k e u)").bitcast(BF16),
+                in_=woven[:].rearrange("p g e x -> p (g e x)").bitcast(BF16),
             )
-            for k in range(n):
+            for k in range(count):
                 v_codes[b, first + k] = codes[:, k * P : (k + 1) * P]
                 v_scales[b, first + k] = scales[:, k * P : (k + 1) * P]
 
-        block(0, ("bank6", "bank7"))
+        woven0 = keep.tile([P, PASSES, P, 2], F32, name="woven0", align_bytes=64)
+        scaled0 = gather(0, 0, I, "scaled0")
+        for g in range(PASSES):
+            round_to_pairs(0, g * KP, (g + 1) * KP, scaled0[:, g * KP : (g + 1) * KP], nc.scalar.copy)
+        for g in range(PASSES):
+            turn_pairs(0, g, "bank%d" % (6 + g), woven0[:, g])
 
         s_sb = keep.tile([P, I], F32, name="s_sb", tag="s_sb", align_bytes=64)
         for g in range(PASSES):
@@ -152,25 +154,31 @@ def tile_attend_beamcache_kernel(tc, query, keys_words, keys_scales, mask, size,
             nc.vector.tensor_tensor(s_sb[:, cols], score_ps[g][:], mask_sb[:, cols], ALU.add)
         neg_max = keep.tile([P, 1], F32, name="neg_max")
         nc.vector.tensor_reduce(neg_max[:], s_sb[:], AX.X, ALU.max, negate=True)
-        p_sb = keep.tile([P, I], F32, name="p_sb", tag="p_sb", align_bytes=64)
+        p_sb = keep.tile([P, I], F32, name="p_sb", align_bytes=64)
         row_sum = keep.tile([P, 1], F32, name="row_sum", tag="row_sum", align_bytes=64)
         nc.scalar.activation(p_sb[:], s_sb[:], ACT.Exp, bias=neg_max[:], accum_out=row_sum[:])
 
-        block(1, ("bank4", "bank5"))
-        inv_sum = keep.tile([P, 1], F32, name="inv_sum", tag="inv_sum", align_bytes=64)
+        woven1 = keep.tile([P, PASSES, P, PACK], BF16, name="woven1", align_bytes=64)
+        scaled1 = gather(1, 0, I, "scaled1")
+        for g in range(PASSES):
+            bank = psum.tile([P, PACK, P], F32, name="turned1%d" % g, tag="bank%d" % (4 + g))
+            for t in range(PACK):
+                nc.tensor.transpose(bank[:, t, :], scaled1[:, g * KP + t : (g + 1) * KP : PACK], ident[:])
+            nc.scalar.copy(woven1[:, g], bank[:].rearrange("p t e -> p e t"))
+        inv_sum = keep.tile([P, 1], F32, name="inv_sum", align_bytes=64)
         nc.vector.reciprocal(inv_sum[:], row_sum[:])
-        woven[2, 0] = keep.tile([P, PASSES, P, 2], F32, name="v_words2", align_bytes=64)
-        early = gather(2, 0, KP, "s_sb")
+        woven2 = keep.tile([P, PASSES, P, 2], F32, name="woven2", align_bytes=64)
+        scaled20 = gather(2, 0, KP, "s_sb")
 
         wt = keep.tile([P, PASSES, Q, 2], F32, name="wt", tag="wt", align_bytes=64)
         for g in range(PASSES):
             cols = slice(g * KP, (g + 1) * KP)
             w_bf = keep.tile([P, KP], BF16, name="w_bf%d" % g, tag="w_bf%d" % g, align_bytes=64)
             nc.vector.scalar_tensor_tensor(
-                w_bf[:].rearrange("p (n t) -> p n t", t=PACK),
-                p_sb[:, cols].rearrange("p (n t) -> p n t", t=PACK),
+                w_bf[:].rearrange("q (n t) -> q n t", t=PACK),
+                p_sb[:, cols].rearrange("q (n t) -> q n t", t=PACK),
                 inv_sum[:],
-                size_ps[g][:].rearrange("p t n -> p n t"),
+                size_ps[g][:].rearrange("q t n -> q n t"),
                 ALU.mult, ALU.mult,
             )
             words = w_bf[:].bitcast(F32)
@@ -179,45 +187,44 @@ def tile_attend_beamcache_kernel(tc, query, keys_words, keys_scales, mask, size,
                 nc.tensor.transpose(bank[:, u, :], words[:, u : KP // 2 : 2], ident[:])
             nc.scalar.copy(wt[:, g], bank[:].rearrange("p u q -> p q u"))
 
-        cast(2, 0, KP, early[:], nc.scalar.copy)
-        turn(2, 0, "bank6", woven[2, 0][:, 0])
-        cast(2, KP, I, gather(2, KP, I, "row_sum")[:], nc.scalar.copy)
-        turn(2, 1, "bank7", woven[2, 0][:, 1])
-        last = BLOCKS - 1
-        cast(last, 0, KP, gather(last, 0, KP, "w_bf0")[:], nc.scalar.copy)
-        w_all = keep.tile([P, PASSES * Q], U32, name="w_codes", align_bytes=64)
-        w_all_scales = keep.tile([P, PASSES * Q], U8, name="w_scales", align_bytes=64)
+        round_to_pairs(2, 0, KP, scaled20[:], nc.scalar.copy)
+        turn_pairs(2, 0, "bank6", woven2[:, 0])
+        round_to_pairs(2, KP, I, gather(2, KP, I, "row_sum")[:], nc.scalar.copy)
+        turn_pairs(2, 1, "bank7", woven2[:, 1])
+        round_to_pairs(LAST, 0, KP, gather(LAST, 0, KP, "w_bf0")[:], nc.scalar.copy)
+        w_codes = keep.tile([P, PASSES * Q], U32, name="w_codes", align_bytes=64)
+        w_scales = keep.tile([P, PASSES * Q], U8, name="w_scales", align_bytes=64)
         nc.vector.quantize_mx(
-            out=w_all[:].bitcast(FP8X4), scales=w_all_scales[:],
+            out=w_codes[:].bitcast(FP8X4), scales=w_scales[:],
             in_=wt[:].rearrange("p g q u -> p (g q u)").bitcast(BF16),
         )
-        w_codes = [w_all[:, g * Q : (g + 1) * Q] for g in range(PASSES)]
-        w_scales = [w_all_scales[:, g * Q : (g + 1) * Q] for g in range(PASSES)]
 
-        cast(last, KP, I - P, gather(last, KP, I - P, "w_bf1")[:], nc.scalar.copy)
-        woven[last, 0] = keep.tile([P, 1, P, 2], F32, name="v_words30", align_bytes=64)
-        woven[last, 1] = keep.tile([P, 1, P, 2], F32, name="v_words31", align_bytes=64)
-        turn(last, 0, "bank4", woven[last, 0][:, 0])
-        cast(last, I - P, I, gather(last, I - P, I, "wt")[:], nc.vector.tensor_copy)
-        turn(last, 1, "bank5", woven[last, 1][:, 0])
-        late_codes = keep.tile([P, 8 * P], U32, name="late_codes", tag="reused", align_bytes=64)
-        for b in range(last):
-            quantize_values(b, 0, 2, late_codes[:, 2 * b * P : 2 * (b + 1) * P])
-        quantize_values(3, 0, 1, late_codes[:, 6 * P : 7 * P])
-        quantize_values(3, 1, 2, late_codes[:, 7 * P : 8 * P])
+        round_to_pairs(LAST, KP, CUT, gather(LAST, KP, CUT, "w_bf1")[:], nc.scalar.copy)
+        woven_last = [keep.tile([P, 1, P, 2], F32, name="woven_last%d" % g, align_bytes=64) for g in range(PASSES)]
+        turn_pairs(LAST, 0, "bank4", woven_last[0][:, 0])
+        round_to_pairs(LAST, CUT, I, gather(LAST, CUT, I, "wt")[:], nc.vector.tensor_copy)
+        turn_pairs(LAST, 1, "bank5", woven_last[1][:, 0])
 
-        for first, last, tag, copy in (
-            (0, 3, "bank4", nc.scalar.copy), (3, 4, "bank1", nc.vector.tensor_copy)
+        all_codes = keep.tile([P, BLOCKS, PASSES * P], U32, name="all_codes", tag="vsc_row", align_bytes=64)
+        for b, woven in enumerate((woven0, woven1, woven2)):
+            quantize_values(b, 0, woven, all_codes[:, b, :])
+        for g in range(PASSES):
+            quantize_values(LAST, g, woven_last[g], all_codes[:, LAST, g * P : (g + 1) * P])
+
+        for first, end, tag, copy in (
+            (0, LAST, "bank4", nc.scalar.copy),
+            (LAST, BLOCKS, "bank1", nc.vector.tensor_copy),
         ):
-            acc = psum.tile([P, (last - first) * P], F32, name="acc%d" % first, tag=tag)
-            for b in range(first, last):
+            acc = psum.tile([P, (end - first) * P], F32, name="acc%d" % first, tag=tag)
+            for b in range(first, end):
                 for g in range(PASSES):
+                    rows = slice(g * Q, (g + 1) * Q)
                     nc.tensor.matmul_mx(
                         out=acc[:, (b - first) * P : (b - first + 1) * P],
-                        lhsT=w_codes[g].bitcast(FP8X4), lhsT_scale=w_scales[g],
+                        lhsT=w_codes[:, rows].bitcast(FP8X4), lhsT_scale=w_scales[:, rows],
                         rhs=v_codes[b, g].bitcast(FP8X4), rhs_scale=v_scales[b, g],
                         start=(g == 0), stop=(g == PASSES - 1),
                     )
-            result = keep.tile([P, (last - first) * P], F32, name="result%d" % first)
+            result = keep.tile([P, (end - first) * P], F32, name="result%d" % first)
             copy(result[:], acc[:])
-            nc.sync.dma_start(out[:, first * P : last * P], result[:])
+            nc.sync.dma_start(out[:, first * P : end * P], result[:])

@@ -108,7 +108,7 @@ def tile_attend_beamcache_kernel(tc, query, keys_words, keys_scales, mask, size,
         v_scales = {}
 
         def gather(b, lo, hi, tag):
-            scaled = keep.tile([P, hi - lo], F32, name="scaled%d_%d" % (b, lo), tag=tag, align_bytes=64)
+            scaled = keep.tile([P, hi - lo], F32, name="scaled%d_%d_%d" % (b, lo, hi), tag=tag, align_bytes=64)
             nc.vector.tensor_tensor(
                 scaled[:], v_pool[b][:].indirect(offsets[:, lo // STRIPE : hi // STRIPE]), vsc_row[:, lo:hi], ALU.mult
             )
@@ -202,7 +202,7 @@ def tile_attend_beamcache_kernel(tc, query, keys_words, keys_scales, mask, size,
         round_to_pairs(LAST, KP, CUT, gather(LAST, KP, CUT, "w_bf1")[:], nc.scalar.copy)
         woven_last = [keep.tile([P, 1, P, 2], F32, name="woven_last%d" % g, align_bytes=64) for g in range(PASSES)]
         turn_pairs(LAST, 0, "bank4", woven_last[0][:, 0])
-        round_to_pairs(LAST, CUT, I, gather(LAST, CUT, I, "wt")[:], nc.vector.tensor_copy)
+        round_to_pairs(LAST, CUT, I, gather(LAST, 0, I, "wt")[:, CUT:I], nc.vector.tensor_copy)
         turn_pairs(LAST, 1, "bank5", woven_last[1][:, 0])
 
         all_codes = keep.tile([P, BLOCKS, PASSES * P], U32, name="all_codes", tag="vsc_row", align_bytes=64)

@@ -26,7 +26,8 @@ LAST = BLOCKS - 1
 STRIPE = 16
 QUADRANT = 32
 PER_ROW = I // P
-CUT = I - 2 * P
+V_AT = (0, 8192)
+ROW_AT = (24576, 26624)
 
 
 def tile_attend_beamcache_kernel(tc, query, keys_words, keys_scales, mask, size, vsc, vals, offs, out):
@@ -35,96 +36,97 @@ def tile_attend_beamcache_kernel(tc, query, keys_words, keys_scales, mask, size,
         keep = ctx.enter_context(tc.tile_pool(name="keep", bufs=1))
         psum = ctx.enter_context(tc.psum_pool(name="psum", bufs=1))
 
+        shared = ctx.enter_context(tc.tile_pool(name="shared", bufs=1))
+
+        def placed(shape, dtype, name, offset):
+            return shared.tile(shape, dtype, name=name, offset=offset, align_bytes=64)
+
+        def sb(shape, dtype, name, tag=None):
+            return keep.tile(shape, dtype, name=name, tag=tag or name, align_bytes=64)
+
         offsets = keep.tile([P, I // STRIPE], U16, name="offsets")
         nc.sync.dma_start(offsets[:], offs)
-        vsc_col = keep.tile([P, PER_ROW], F32, name="vsc_col")
+        vsc_col = sb([P, PER_ROW], F32, "vsc_col")
         nc.scalar.dma_start(vsc_col[:], vsc.rearrange("(n c) o -> n (c o)", c=PER_ROW))
-        size_col = keep.tile([P, PASSES, 2 * PACK], F32, name="size_col")
-        nc.scalar.dma_start(size_col[:, :, 0:PACK], size.rearrange("o (g p t) -> p (o g) t", g=PASSES, t=PACK))
-        kw_pool = keep.tile([P, T], I32, name="kw_pool", align_bytes=64)
+        kw_pool = sb([P, T], I32, "kw_pool")
         nc.sync.dma_start(kw_pool[:], keys_words[0].rearrange("p n t -> p (n t)").bitcast(I32))
-        ks_pool = keep.tile([P, T], U8, name="ks_pool", align_bytes=64)
+        q_raw = sb([P, PACK, Q], F32, "q_raw")
+        nc.sync.dma_start(q_raw[:], query.rearrange("(p t) q -> p t q", t=PACK))
+        ks_pool = sb([P, T], U8, "ks_pool")
         nc.vector.memset(ks_pool[:].bitcast(I32), 0)
         for r in range(PACK):
             nc.sync.dma_start(
                 ks_pool[r:P:QUADRANT, :].bitcast(I32), keys_scales[0, r : KP // QUADRANT : PACK, :].bitcast(I32)
             )
-        q_raw = keep.tile([P, PACK, Q], F32, name="q_raw")
-        nc.sync.dma_start(q_raw[:], query.rearrange("(p t) q -> p t q", t=PACK))
-        v_pool = [keep.tile([P, T], F32, name="v_pool%d" % b, align_bytes=64) for b in range(BLOCKS)]
+        v_pool = [placed([P, T], F32, "v_pool%d" % b, V_AT[b]) for b in range(2)]
+        v_pool.extend(sb([P, T], F32, "v_pool%d" % b) for b in range(2, BLOCKS))
         nc.sync.dma_start(v_pool[0][:], vals[0:P, :])
-        mask_sb = keep.tile([P, I], F32, name="mask_sb")
+        mask_sb = sb([P, I], F32, "mask_sb")
         nc.sync.dma_start(mask_sb[:], mask)
+        size_col = sb([P, PASSES, 2 * PACK], F32, "size_col")
+        nc.sync.dma_start(size_col[:, :, 0:PACK], size.rearrange("o (g p t) -> p (o g) t", g=PASSES, t=PACK))
         for b in range(1, BLOCKS):
             nc.sync.dma_start(v_pool[b][:], vals[b * P : (b + 1) * P, :])
 
         ident = keep.tile([P, P], F32, name="ident")
         make_identity(nc, ident[:])
 
-        kw = keep.tile([P, I], U32, name="kw", align_bytes=64)
+        def cols(g):
+            return slice(g * KP, (g + 1) * KP)
+
+        def listed(g):
+            return offsets[:, g * KP // STRIPE : (g + 1) * KP // STRIPE]
+
+        kw = sb([P, I], U32, "kw")
         nc.vector.tensor_copy(kw[:], kw_pool[:].bitcast(U32).indirect(offsets[:]))
-
-        vsc_row = keep.tile([P, I], F32, name="vsc_row", tag="vsc_row", align_bytes=64)
-        for half in range(PER_ROW // PACK):
-            bank = psum.tile([P, PACK, P], F32, name="vsc_ps%d" % half, tag="bank%d" % (4 + half))
-            for c in range(PACK):
-                column = half * PACK + c
-                nc.tensor.transpose(bank[:, c, :], vsc_col[:, column : column + 1].to_broadcast([P, P]), ident[:])
-            nc.scalar.copy(
-                vsc_row[:].rearrange("p (n c) -> p n c", c=PER_ROW)[:, :, half * PACK : (half + 1) * PACK],
-                bank[:].rearrange("p c n -> p n c"),
-            )
-
-        q_bf = keep.tile([P, Q, PACK], BF16, name="q_bf", align_bytes=64)
+        q_bf = sb([P, Q, PACK], BF16, "q_bf")
         nc.scalar.copy(q_bf[:], q_raw[:].rearrange("p t q -> p q t"))
-        q_codes = keep.tile([P, Q], U32, name="q_codes", align_bytes=64)
-        q_scales = keep.tile([P, Q], U8, name="q_scales", align_bytes=64)
+        q_codes = sb([P, Q], U32, "q_codes")
+        q_scales = sb([P, Q], U8, "q_scales")
         nc.vector.quantize_mx(
             out=q_codes[:].bitcast(FP8X4), scales=q_scales[:], in_=q_bf[:].rearrange("p q t -> p (q t)")
         )
-
-        ks = keep.tile([P, I], U8, name="ks", align_bytes=64)
+        ks = sb([P, I], U8, "ks", "q_raw")
         nc.vector.tensor_copy(ks[:], ks_pool[:].indirect(offsets[:]))
 
-        size_ps = []
-        for g in range(PASSES):
-            bank = psum.tile([P, PACK, P], F32, name="size_ps%d" % g, tag="bank%d" % g)
-            for t in range(PACK):
-                nc.tensor.transpose(bank[:, t, :], size_col[:, g, t : t + 1].to_broadcast([P, P]), ident[:])
-            size_ps.append(bank)
+        def spread_turns(column, name, first_bank):
+            banks = []
+            for half in range(PER_ROW // PACK):
+                bank = psum.tile([P, PACK, P], F32, name="%s_ps%d" % (name, half), tag="bank%d" % (first_bank + half))
+                for c in range(PACK):
+                    k = half * PACK + c
+                    nc.tensor.transpose(bank[:, c, :], column[:, k : k + 1].to_broadcast([P, P]), ident[:])
+                banks.append(bank)
+            return banks
 
-        score_ps = []
-        for g in range(PASSES):
-            cols = slice(g * KP, (g + 1) * KP)
-            bank = psum.tile([P, KP], F32, name="score_ps%d" % g, tag="bank%d" % (2 + g))
-            nc.tensor.matmul_mx(
-                out=bank[:], lhsT=q_codes[:].bitcast(FP8X4), lhsT_scale=q_scales[:],
-                rhs=kw[:, cols].bitcast(FP8X4), rhs_scale=ks[:, cols], start=True, stop=True,
-            )
-            score_ps.append(bank)
+        def spread_copies(banks, rows):
+            for g in range(PASSES):
+                for half, bank in enumerate(banks):
+                    nc.scalar.copy(
+                        rows[g][:].rearrange("p (n c) -> p n c", c=PER_ROW)[:, :, half * PACK : (half + 1) * PACK],
+                        bank[:, :, g * P // PASSES : (g + 1) * P // PASSES].rearrange("p c n -> p n c"),
+                    )
+            return rows
 
-        pairs = {}
+        vsc_banks = spread_turns(vsc_col, "vsc", 0)
+
+        vsc_row = spread_copies(
+            vsc_banks, [placed([P, KP], F32, "vsc_row%d" % g, ROW_AT[g]) for g in range(PASSES)]
+        )
+
         v_codes = {}
         v_scales = {}
 
-        def gather(b, lo, hi, tag):
-            scaled = keep.tile([P, hi - lo], F32, name="scaled%d_%d_%d" % (b, lo, hi), tag=tag, align_bytes=64)
-            nc.vector.tensor_tensor(
-                scaled[:], v_pool[b][:].indirect(offsets[:, lo // STRIPE : hi // STRIPE]), vsc_row[:, lo:hi], ALU.mult
-            )
-            return scaled
+        def gather(b, g, scaled):
+            nc.vector.tensor_tensor(scaled, v_pool[b][:].indirect(listed(g)), vsc_row[g][:], ALU.mult)
 
-        def round_to_pairs(b, lo, hi, scaled, copy):
-            g = lo // KP
-            if (b, g) not in pairs:
-                pairs[b, g] = keep.tile([P, 2, P, 2], BF16, name="pairs%d%d" % (b, g), align_bytes=64)
-            copy(
-                pairs[b, g][:, :, (lo - g * KP) // PACK : (hi - g * KP) // PACK, :],
-                scaled.rearrange("e (n u h) -> e u n h", u=2, h=2),
-            )
+        def round_to_pairs(b, g, scaled, copy):
+            pairs = sb([P, 2, P, 2], BF16, "pairs%d%d" % (b, g))
+            copy(pairs[:], scaled.rearrange("e (n u h) -> e u n h", u=2, h=2))
+            return pairs
 
-        def turn_pairs(b, g, bank_tag, woven):
-            words = pairs[b, g][:].rearrange("e u n h -> e (u n h)").bitcast(F32)
+        def turn_pairs(b, g, pairs, bank_tag, woven):
+            words = pairs[:].rearrange("e u n h -> e (u n h)").bitcast(F32)
             bank = psum.tile([P, 2, P], F32, name="turned%d%d" % (b, g), tag=bank_tag)
             for u in range(2):
                 nc.tensor.transpose(bank[:, u, :], words[:, u * P : (u + 1) * P], ident[:])
@@ -132,7 +134,7 @@ def tile_attend_beamcache_kernel(tc, query, keys_words, keys_scales, mask, size,
 
         def quantize_values(b, first, woven, codes):
             count = woven.shape[1]
-            scales = keep.tile([P, count * P], U8, name="v_scales%d%d" % (b, first), align_bytes=64)
+            scales = sb([P, count * P], U8, "v_scales%d%d" % (b, first))
             nc.vector.quantize_mx(
                 out=codes.bitcast(FP8X4), scales=scales[:],
                 in_=woven[:].rearrange("p g e x -> p (g e x)").bitcast(BF16),
@@ -141,42 +143,56 @@ def tile_attend_beamcache_kernel(tc, query, keys_words, keys_scales, mask, size,
                 v_codes[b, first + k] = codes[:, k * P : (k + 1) * P]
                 v_scales[b, first + k] = scales[:, k * P : (k + 1) * P]
 
-        woven0 = keep.tile([P, PASSES, P, 2], F32, name="woven0", align_bytes=64)
-        scaled0 = gather(0, 0, I, "scaled0")
+        scaled0 = sb([P, I], F32, "scaled0")
+        pairs0 = []
         for g in range(PASSES):
-            round_to_pairs(0, g * KP, (g + 1) * KP, scaled0[:, g * KP : (g + 1) * KP], nc.scalar.copy)
+            gather(0, g, scaled0[:, cols(g)])
+            pairs0.append(round_to_pairs(0, g, scaled0[:, cols(g)], nc.scalar.copy))
+        woven0 = placed([P, PASSES, P, 2], F32, "woven0", V_AT[0])
         for g in range(PASSES):
-            turn_pairs(0, g, "bank%d" % (6 + g), woven0[:, g])
+            turn_pairs(0, g, pairs0[g], "bank%d" % (6 + g), woven0[:, g])
 
-        s_sb = keep.tile([P, I], F32, name="s_sb", tag="s_sb", align_bytes=64)
+        s_sb = sb([P, I], F32, "s_sb")
         for g in range(PASSES):
-            cols = slice(g * KP, (g + 1) * KP)
-            nc.vector.tensor_tensor(s_sb[:, cols], score_ps[g][:], mask_sb[:, cols], ALU.add)
-        neg_max = keep.tile([P, 1], F32, name="neg_max")
+            bank = psum.tile([P, KP], F32, name="score_ps%d" % g, tag="bank%d" % (4 + g))
+            nc.tensor.matmul_mx(
+                out=bank[:], lhsT=q_codes[:].bitcast(FP8X4), lhsT_scale=q_scales[:],
+                rhs=kw[:, cols(g)].bitcast(FP8X4), rhs_scale=ks[:, cols(g)], start=True, stop=True,
+            )
+            nc.vector.tensor_tensor(s_sb[:, cols(g)], bank[:], mask_sb[:, cols(g)], ALU.add)
+        size_ps = []
+        for g in range(PASSES):
+            bank = psum.tile([P, PACK, P], F32, name="size_ps%d" % g, tag="bank%d" % (4 + g))
+            for t in range(PACK):
+                nc.tensor.transpose(bank[:, t, :], size_col[:, g, t : t + 1].to_broadcast([P, P]), ident[:])
+            size_ps.append(bank)
+
+        neg_max = sb([P, 1], F32, "neg_max")
         nc.vector.tensor_reduce(neg_max[:], s_sb[:], AX.X, ALU.max, negate=True)
-        p_sb = keep.tile([P, I], F32, name="p_sb", align_bytes=64)
-        row_sum = keep.tile([P, 1], F32, name="row_sum", tag="row_sum", align_bytes=64)
+        p_sb = sb([P, I], F32, "p_sb")
+        row_sum = sb([P, 1], F32, "row_sum")
         nc.scalar.activation(p_sb[:], s_sb[:], ACT.Exp, bias=neg_max[:], accum_out=row_sum[:])
 
-        woven1 = keep.tile([P, PASSES, P, PACK], BF16, name="woven1", align_bytes=64)
-        scaled1 = gather(1, 0, I, "scaled1")
-        for g in range(PASSES):
-            bank = psum.tile([P, PACK, P], F32, name="turned1%d" % g, tag="bank%d" % (4 + g))
-            for t in range(PACK):
-                nc.tensor.transpose(bank[:, t, :], scaled1[:, g * KP + t : (g + 1) * KP : PACK], ident[:])
-            nc.scalar.copy(woven1[:, g], bank[:].rearrange("p t e -> p e t"))
-        inv_sum = keep.tile([P, 1], F32, name="inv_sum", align_bytes=64)
-        nc.vector.reciprocal(inv_sum[:], row_sum[:])
-        woven2 = keep.tile([P, PASSES, P, 2], F32, name="woven2", align_bytes=64)
-        scaled20 = gather(2, 0, KP, "s_sb")
 
-        wt = keep.tile([P, PASSES, Q, 2], F32, name="wt", tag="wt", align_bytes=64)
+        scaled1 = sb([P, I], F32, "scaled1", "mask_sb")
+        pairs1 = []
         for g in range(PASSES):
-            cols = slice(g * KP, (g + 1) * KP)
-            w_bf = keep.tile([P, KP], BF16, name="w_bf%d" % g, tag="w_bf%d" % g, align_bytes=64)
+            gather(1, g, scaled1[:, cols(g)])
+            pairs1.append(round_to_pairs(1, g, scaled1[:, cols(g)], nc.scalar.copy))
+        woven1 = placed([P, PASSES, P, 2], F32, "woven1", V_AT[1])
+        for g in range(PASSES):
+            turn_pairs(1, g, pairs1[g], "bank%d" % g, woven1[:, g])
+
+        inv_sum = placed([P, 1], F32, "inv_sum", V_AT[1] + 2048)
+        nc.vector.reciprocal(inv_sum[:], row_sum[:])
+        quantize_values(0, 0, woven0, placed([P, PASSES * P], U32, "codes0", V_AT[1] + 4096)[:])
+
+        wt = sb([P, PASSES, Q, 2], F32, "wt")
+        for g in range(PASSES):
+            w_bf = sb([P, KP], BF16, "w_bf%d" % g)
             nc.vector.scalar_tensor_tensor(
                 w_bf[:].rearrange("q (n t) -> q n t", t=PACK),
-                p_sb[:, cols].rearrange("q (n t) -> q n t", t=PACK),
+                p_sb[:, cols(g)].rearrange("q (n t) -> q n t", t=PACK),
                 inv_sum[:],
                 size_ps[g][:].rearrange("q t n -> q n t"),
                 ALU.mult, ALU.mult,
@@ -187,33 +203,38 @@ def tile_attend_beamcache_kernel(tc, query, keys_words, keys_scales, mask, size,
                 nc.tensor.transpose(bank[:, u, :], words[:, u : KP // 2 : 2], ident[:])
             nc.scalar.copy(wt[:, g], bank[:].rearrange("p u q -> p q u"))
 
-        round_to_pairs(2, 0, KP, scaled20[:], nc.scalar.copy)
-        turn_pairs(2, 0, "bank6", woven2[:, 0])
-        round_to_pairs(2, KP, I, gather(2, KP, I, "row_sum")[:], nc.scalar.copy)
-        turn_pairs(2, 1, "bank7", woven2[:, 1])
-        round_to_pairs(LAST, 0, KP, gather(LAST, 0, KP, "w_bf0")[:], nc.scalar.copy)
-        w_codes = keep.tile([P, PASSES * Q], U32, name="w_codes", align_bytes=64)
-        w_scales = keep.tile([P, PASSES * Q], U8, name="w_scales", align_bytes=64)
+        pairs2 = []
+        scaled2 = sb([P, I], F32, "scaled2", "row_sum")
+        for g in range(PASSES):
+            gather(2, g, scaled2[:, cols(g)])
+            pairs2.append(round_to_pairs(2, g, scaled2[:, cols(g)], nc.scalar.copy))
+
+        scaled3 = sb([P, I], F32, "scaled3", "p_sb")
+        gather(LAST, 0, scaled3[:, cols(0)])
+        pairs30 = round_to_pairs(LAST, 0, scaled3[:, cols(0)], nc.scalar.copy)
+        gather(LAST, 1, scaled3[:, cols(1)])
+        woven2 = placed([P, PASSES, P, 2], F32, "woven2", ROW_AT[0] + 64 - 2048)
+        for g in range(PASSES):
+            turn_pairs(2, g, pairs2[g], "bank%d" % (4 + g), woven2[:, g])
+        woven_last = [sb([P, 1, P, 2], F32, "woven_last%d" % g) for g in range(PASSES)]
+        turn_pairs(LAST, 0, pairs30, "bank6", woven_last[0][:, 0])
+        w_codes = placed([P, PASSES * Q], U32, "w_codes", ROW_AT[0] + 64)
+        w_scales = sb([P, PASSES * Q], U8, "w_scales")
         nc.vector.quantize_mx(
             out=w_codes[:].bitcast(FP8X4), scales=w_scales[:],
             in_=wt[:].rearrange("p g q u -> p (g q u)").bitcast(BF16),
         )
-
-        round_to_pairs(LAST, KP, CUT, gather(LAST, KP, CUT, "w_bf1")[:], nc.scalar.copy)
-        woven_last = [keep.tile([P, 1, P, 2], F32, name="woven_last%d" % g, align_bytes=64) for g in range(PASSES)]
-        turn_pairs(LAST, 0, "bank4", woven_last[0][:, 0])
-        round_to_pairs(LAST, CUT, I, gather(LAST, 0, I, "wt")[:, CUT:I], nc.vector.tensor_copy)
-        turn_pairs(LAST, 1, "bank5", woven_last[1][:, 0])
-
-        all_codes = keep.tile([P, BLOCKS, PASSES * P], U32, name="all_codes", tag="vsc_row", align_bytes=64)
-        for b, woven in enumerate((woven0, woven1, woven2)):
-            quantize_values(b, 0, woven, all_codes[:, b, :])
+        pairs = round_to_pairs(LAST, 1, scaled3[:, cols(1)], nc.vector.tensor_copy)
+        turn_pairs(LAST, 1, pairs, "bank7", woven_last[1][:, 0])
+        late_codes = placed([P, LAST, PASSES * P], U32, "late_codes", ROW_AT[1])
+        quantize_values(1, 0, woven1, late_codes[:, 0, :])
+        quantize_values(2, 0, woven2, late_codes[:, 1, :])
         for g in range(PASSES):
-            quantize_values(LAST, g, woven_last[g], all_codes[:, LAST, g * P : (g + 1) * P])
+            quantize_values(LAST, g, woven_last[g], late_codes[:, 2, g * P : (g + 1) * P])
 
         for first, end, tag, copy in (
-            (0, LAST, "bank4", nc.scalar.copy),
-            (LAST, BLOCKS, "bank1", nc.vector.tensor_copy),
+            (0, LAST, "bank6", nc.scalar.copy),
+            (LAST, BLOCKS, "bank0", nc.vector.tensor_copy),
         ):
             acc = psum.tile([P, (end - first) * P], F32, name="acc%d" % first, tag=tag)
             for b in range(first, end):
@@ -225,6 +246,6 @@ def tile_attend_beamcache_kernel(tc, query, keys_words, keys_scales, mask, size,
                         rhs=v_codes[b, g].bitcast(FP8X4), rhs_scale=v_scales[b, g],
                         start=(g == 0), stop=(g == PASSES - 1),
                     )
-            result = keep.tile([P, (end - first) * P], F32, name="result%d" % first)
+            result = sb([P, (end - first) * P], F32, "result%d" % first)
             copy(result[:], acc[:])
             nc.sync.dma_start(out[:, first * P : end * P], result[:])

@@ -26,8 +26,8 @@ LAST = BLOCKS - 1
 STRIPE = 16
 QUADRANT = 32
 PER_ROW = I // P
-V_AT = (0, 8192)
-ROW_AT = (24576, 26624)
+V_AT = (0, 8192, 16384)
+ROW_AT = (24576, 30720)
 
 
 def tile_attend_beamcache_kernel(tc, query, keys_words, keys_scales, mask, size, vsc, vals, offs, out):
@@ -48,6 +48,8 @@ def tile_attend_beamcache_kernel(tc, query, keys_words, keys_scales, mask, size,
         nc.sync.dma_start(offsets[:], offs)
         vsc_col = sb([P, PER_ROW], F32, "vsc_col")
         nc.scalar.dma_start(vsc_col[:], vsc.rearrange("(n c) o -> n (c o)", c=PER_ROW))
+        size_col = sb([P, PASSES, 2 * PACK], F32, "size_col")
+        nc.scalar.dma_start(size_col[:, :, 0:PACK], size.rearrange("o (g p t) -> p (o g) t", g=PASSES, t=PACK))
         kw_pool = sb([P, T], I32, "kw_pool")
         nc.sync.dma_start(kw_pool[:], keys_words[0].rearrange("p n t -> p (n t)").bitcast(I32))
         q_raw = sb([P, PACK, Q], F32, "q_raw")
@@ -58,13 +60,11 @@ def tile_attend_beamcache_kernel(tc, query, keys_words, keys_scales, mask, size,
             nc.sync.dma_start(
                 ks_pool[r:P:QUADRANT, :].bitcast(I32), keys_scales[0, r : KP // QUADRANT : PACK, :].bitcast(I32)
             )
-        v_pool = [placed([P, T], F32, "v_pool%d" % b, V_AT[b]) for b in range(2)]
-        v_pool.extend(sb([P, T], F32, "v_pool%d" % b) for b in range(2, BLOCKS))
+        v_pool = [placed([P, T], F32, "v_pool%d" % b, V_AT[b]) for b in range(LAST)]
+        v_pool.append(sb([P, T], F32, "v_pool%d" % LAST))
         nc.sync.dma_start(v_pool[0][:], vals[0:P, :])
         mask_sb = sb([P, I], F32, "mask_sb")
         nc.sync.dma_start(mask_sb[:], mask)
-        size_col = sb([P, PASSES, 2 * PACK], F32, "size_col")
-        nc.sync.dma_start(size_col[:, :, 0:PACK], size.rearrange("o (g p t) -> p (o g) t", g=PASSES, t=PACK))
         for b in range(1, BLOCKS):
             nc.sync.dma_start(v_pool[b][:], vals[b * P : (b + 1) * P, :])
 
@@ -187,7 +187,7 @@ def tile_attend_beamcache_kernel(tc, query, keys_words, keys_scales, mask, size,
         nc.vector.reciprocal(inv_sum[:], row_sum[:])
         quantize_values(0, 0, woven0, placed([P, PASSES * P], U32, "codes0", V_AT[1] + 4096)[:])
 
-        wt = sb([P, PASSES, Q, 2], F32, "wt")
+        w_ps = psum.tile([P, PASSES, 2, Q], F32, name="w_ps", tag="bank2")
         for g in range(PASSES):
             w_bf = sb([P, KP], BF16, "w_bf%d" % g)
             nc.vector.scalar_tensor_tensor(
@@ -198,42 +198,46 @@ def tile_attend_beamcache_kernel(tc, query, keys_words, keys_scales, mask, size,
                 ALU.mult, ALU.mult,
             )
             words = w_bf[:].bitcast(F32)
-            bank = psum.tile([P, 2, Q], F32, name="w_ps%d" % g, tag="bank%d" % (2 + g))
             for u in range(2):
-                nc.tensor.transpose(bank[:, u, :], words[:, u : KP // 2 : 2], ident[:])
-            nc.scalar.copy(wt[:, g], bank[:].rearrange("p u q -> p q u"))
+                nc.tensor.transpose(w_ps[:, g, u, :], words[:, u : KP // 2 : 2], ident[:])
 
         pairs2 = []
         scaled2 = sb([P, I], F32, "scaled2", "row_sum")
         for g in range(PASSES):
             gather(2, g, scaled2[:, cols(g)])
             pairs2.append(round_to_pairs(2, g, scaled2[:, cols(g)], nc.scalar.copy))
+        wt = placed([P, PASSES, Q, 2], F32, "wt", V_AT[2])
+        nc.scalar.copy(wt[:], w_ps[:].rearrange("p g u q -> p g q u"))
+        woven2 = sb([P, PASSES, P, 2], F32, "woven2")
+        turned2 = psum.tile([P, PASSES, 2, P], F32, name="turned2", tag="bank3")
+        for g in range(PASSES):
+            words = pairs2[g][:].rearrange("e u n h -> e (u n h)").bitcast(F32)
+            for u in range(2):
+                nc.tensor.transpose(turned2[:, g, u, :], words[:, u * P : (u + 1) * P], ident[:])
+        nc.scalar.copy(woven2[:], turned2[:].rearrange("p g u e -> p g e u"))
 
         scaled3 = sb([P, I], F32, "scaled3", "p_sb")
-        gather(LAST, 0, scaled3[:, cols(0)])
-        pairs30 = round_to_pairs(LAST, 0, scaled3[:, cols(0)], nc.scalar.copy)
-        gather(LAST, 1, scaled3[:, cols(1)])
-        woven2 = placed([P, PASSES, P, 2], F32, "woven2", ROW_AT[0] + 64 - 2048)
         for g in range(PASSES):
-            turn_pairs(2, g, pairs2[g], "bank%d" % (4 + g), woven2[:, g])
+            gather(LAST, g, scaled3[:, cols(g)])
         woven_last = [sb([P, 1, P, 2], F32, "woven_last%d" % g) for g in range(PASSES)]
-        turn_pairs(LAST, 0, pairs30, "bank6", woven_last[0][:, 0])
-        w_codes = placed([P, PASSES * Q], U32, "w_codes", ROW_AT[0] + 64)
+        for g in range(PASSES):
+            pairs = placed([P, 2, P, 2], BF16, "pairs3%d" % g, ROW_AT[0] + 1024 * g)
+            nc.vector.tensor_copy(pairs[:], scaled3[:, cols(g)].rearrange("e (n u h) -> e u n h", u=2, h=2))
+            turn_pairs(LAST, g, pairs, "bank%d" % (6 + g), woven_last[g][:, 0])
+        w_codes = placed([P, PASSES * Q], U32, "w_codes", ROW_AT[1] + 1024)
         w_scales = sb([P, PASSES * Q], U8, "w_scales")
         nc.vector.quantize_mx(
             out=w_codes[:].bitcast(FP8X4), scales=w_scales[:],
             in_=wt[:].rearrange("p g q u -> p (g q u)").bitcast(BF16),
         )
-        pairs = round_to_pairs(LAST, 1, scaled3[:, cols(1)], nc.vector.tensor_copy)
-        turn_pairs(LAST, 1, pairs, "bank7", woven_last[1][:, 0])
-        late_codes = placed([P, LAST, PASSES * P], U32, "late_codes", ROW_AT[1])
+        late_codes = placed([P, LAST, PASSES * P], U32, "late_codes", ROW_AT[1] + 64 - 3072)
         quantize_values(1, 0, woven1, late_codes[:, 0, :])
         quantize_values(2, 0, woven2, late_codes[:, 1, :])
         for g in range(PASSES):
             quantize_values(LAST, g, woven_last[g], late_codes[:, 2, g * P : (g + 1) * P])
 
         for first, end, tag, copy in (
-            (0, LAST, "bank6", nc.scalar.copy),
+            (0, LAST, "bank1", nc.scalar.copy),
             (LAST, BLOCKS, "bank0", nc.vector.tensor_copy),
         ):
             acc = psum.tile([P, (end - first) * P], F32, name="acc%d" % first, tag=tag)

@@ -100,7 +100,7 @@ def tile_attend_beamcache_kernel(tc, query, keys_words, keys_scales, mask, size,
             return banks
 
         def spread_copies(banks, rows):
-            for g in range(PASSES):
+            for g in range(len(rows)):
                 for half, bank in enumerate(banks):
                     nc.scalar.copy(
                         rows[g][:].rearrange("p (n c) -> p n c", c=PER_ROW)[:, :, half * PACK : (half + 1) * PACK],
@@ -114,11 +114,13 @@ def tile_attend_beamcache_kernel(tc, query, keys_words, keys_scales, mask, size,
             vsc_banks, [placed([P, KP], F32, "vsc_row%d" % g, ROW_AT[g]) for g in range(PASSES)]
         )
 
+        vsc_once = spread_copies(vsc_banks, [sb([P, KP], F32, "vsc_once")])[0]
         v_codes = {}
         v_scales = {}
 
         def gather(b, g, scaled):
-            nc.vector.tensor_tensor(scaled, v_pool[b][:].indirect(listed(g)), vsc_row[g][:], ALU.mult)
+            vsc_here = vsc_once if (b, g) == (2, 0) else vsc_row[g]
+            nc.vector.tensor_tensor(scaled, v_pool[b][:].indirect(listed(g)), vsc_here[:], ALU.mult)
 
         def round_to_pairs(b, g, scaled, copy):
             pairs = sb([P, 2, P, 2], BF16, "pairs%d%d" % (b, g))
@@ -131,6 +133,14 @@ def tile_attend_beamcache_kernel(tc, query, keys_words, keys_scales, mask, size,
             for u in range(2):
                 nc.tensor.transpose(bank[:, u, :], words[:, u * P : (u + 1) * P], ident[:])
             nc.scalar.copy(woven, bank[:].rearrange("p u e -> p e u"))
+
+        def turn_block(b, pairs, bank_tag, woven):
+            bank = psum.tile([P, PASSES, 2, P], F32, name="turned%d" % b, tag=bank_tag)
+            for g in range(PASSES):
+                words = pairs[g][:].rearrange("e u n h -> e (u n h)").bitcast(F32)
+                for u in range(2):
+                    nc.tensor.transpose(bank[:, g, u, :], words[:, u * P : (u + 1) * P], ident[:])
+            nc.scalar.copy(woven[:], bank[:].rearrange("p g u e -> p g e u"))
 
         def quantize_values(b, first, woven, codes):
             count = woven.shape[1]
@@ -179,44 +189,37 @@ def tile_attend_beamcache_kernel(tc, query, keys_words, keys_scales, mask, size,
         for g in range(PASSES):
             gather(1, g, scaled1[:, cols(g)])
             pairs1.append(round_to_pairs(1, g, scaled1[:, cols(g)], nc.scalar.copy))
-        woven1 = placed([P, PASSES, P, 2], F32, "woven1", V_AT[1])
-        for g in range(PASSES):
-            turn_pairs(1, g, pairs1[g], "bank%d" % g, woven1[:, g])
-
+        quantize_values(0, 0, woven0, placed([P, PASSES * P], U32, "codes0", V_AT[1] + 4096)[:])
         inv_sum = placed([P, 1], F32, "inv_sum", V_AT[1] + 2048)
         nc.vector.reciprocal(inv_sum[:], row_sum[:])
-        quantize_values(0, 0, woven0, placed([P, PASSES * P], U32, "codes0", V_AT[1] + 4096)[:])
+
+        pairs2 = []
+        scaled2 = sb([P, I], F32, "scaled2", "s_sb")
+        for g in range(PASSES):
+            gather(2, g, scaled2[:, cols(g)])
+            pairs2.append(round_to_pairs(2, g, scaled2[:, cols(g)], nc.scalar.copy))
+        woven1 = placed([P, PASSES, P, 2], F32, "woven1", V_AT[2])
+        turn_block(1, pairs1, "bank0", woven1)
+        woven2 = sb([P, PASSES, P, 2], F32, "woven2")
+        turn_block(2, pairs2, "bank3", woven2)
 
         w_ps = psum.tile([P, PASSES, 2, Q], F32, name="w_ps", tag="bank2")
+        w_bf = sb([P, I], BF16, "w_bf", "vsc_once")
         for g in range(PASSES):
-            w_bf = sb([P, KP], BF16, "w_bf%d" % g)
             nc.vector.scalar_tensor_tensor(
-                w_bf[:].rearrange("q (n t) -> q n t", t=PACK),
+                w_bf[:, cols(g)].rearrange("q (n t) -> q n t", t=PACK),
                 p_sb[:, cols(g)].rearrange("q (n t) -> q n t", t=PACK),
                 inv_sum[:],
                 size_ps[g][:].rearrange("q t n -> q n t"),
                 ALU.mult, ALU.mult,
             )
-            words = w_bf[:].bitcast(F32)
+            words = w_bf[:, cols(g)].bitcast(F32)
             for u in range(2):
                 nc.tensor.transpose(w_ps[:, g, u, :], words[:, u : KP // 2 : 2], ident[:])
-
-        pairs2 = []
-        scaled2 = sb([P, I], F32, "scaled2", "row_sum")
-        for g in range(PASSES):
-            gather(2, g, scaled2[:, cols(g)])
-            pairs2.append(round_to_pairs(2, g, scaled2[:, cols(g)], nc.scalar.copy))
-        wt = placed([P, PASSES, Q, 2], F32, "wt", V_AT[2])
+        wt = sb([P, PASSES, Q, 2], F32, "wt")
         nc.scalar.copy(wt[:], w_ps[:].rearrange("p g u q -> p g q u"))
-        woven2 = sb([P, PASSES, P, 2], F32, "woven2")
-        turned2 = psum.tile([P, PASSES, 2, P], F32, name="turned2", tag="bank3")
-        for g in range(PASSES):
-            words = pairs2[g][:].rearrange("e u n h -> e (u n h)").bitcast(F32)
-            for u in range(2):
-                nc.tensor.transpose(turned2[:, g, u, :], words[:, u * P : (u + 1) * P], ident[:])
-        nc.scalar.copy(woven2[:], turned2[:].rearrange("p g u e -> p g e u"))
 
-        scaled3 = sb([P, I], F32, "scaled3", "p_sb")
+        scaled3 = placed([P, I], F32, "scaled3", V_AT[2] + 4096)
         for g in range(PASSES):
             gather(LAST, g, scaled3[:, cols(g)])
         woven_last = [sb([P, 1, P, 2], F32, "woven_last%d" % g) for g in range(PASSES)]
@@ -237,7 +240,8 @@ def tile_attend_beamcache_kernel(tc, query, keys_words, keys_scales, mask, size,
             quantize_values(LAST, g, woven_last[g], late_codes[:, 2, g * P : (g + 1) * P])
 
         for first, end, tag, copy in (
-            (0, LAST, "bank1", nc.scalar.copy),
+            (0, 2, "bank1", nc.scalar.copy),
+            (2, LAST, "bank4", nc.scalar.copy),
             (LAST, BLOCKS, "bank0", nc.vector.tensor_copy),
         ):
             acc = psum.tile([P, (end - first) * P], F32, name="acc%d" % first, tag=tag)

@@ -46,12 +46,12 @@ def tile_attend_beamcache_kernel(tc, query, keys_words, keys_scales, mask, size,
 
         offsets = keep.tile([P, I // STRIPE], U16, name="offsets")
         nc.sync.dma_start(offsets[:], offs)
-        vsc_col = sb([P, PER_ROW], F32, "vsc_col")
-        nc.scalar.dma_start(vsc_col[:], vsc.rearrange("(n c) o -> n (c o)", c=PER_ROW))
-        size_col = sb([P, PASSES, 2 * PACK], F32, "size_col")
-        nc.scalar.dma_start(size_col[:, :, 0:PACK], size.rearrange("o (g p t) -> p (o g) t", g=PASSES, t=PACK))
         kw_pool = sb([P, T], I32, "kw_pool")
         nc.sync.dma_start(kw_pool[:], keys_words[0].rearrange("p n t -> p (n t)").bitcast(I32))
+        staged = [sb([P, P], F32, "staged%d" % k) for k in range(2)]
+        nc.vector.memset(staged[0][:], 0.0)
+        nc.gpsimd.memset(staged[1][:], 0.0)
+        nc.sync.dma_start(staged[0][0:PER_ROW, :], vsc.rearrange("(c n) o -> c (n o)", n=P))
         q_raw = sb([P, PACK, Q], F32, "q_raw")
         nc.sync.dma_start(q_raw[:], query.rearrange("(p t) q -> p t q", t=PACK))
         ks_pool = sb([P, T], U8, "ks_pool")
@@ -63,6 +63,7 @@ def tile_attend_beamcache_kernel(tc, query, keys_words, keys_scales, mask, size,
         v_pool = [placed([P, T], F32, "v_pool%d" % b, V_AT[b]) for b in range(LAST)]
         v_pool.append(sb([P, T], F32, "v_pool%d" % LAST))
         nc.sync.dma_start(v_pool[0][:], vals[0:P, :])
+        nc.sync.dma_start(staged[1][0:PER_ROW, :], size.rearrange("o (c n) -> (o c) n", n=P))
         mask_sb = sb([P, I], F32, "mask_sb")
         nc.sync.dma_start(mask_sb[:], mask)
         for b in range(1, BLOCKS):
@@ -89,32 +90,29 @@ def tile_attend_beamcache_kernel(tc, query, keys_words, keys_scales, mask, size,
         ks = sb([P, I], U8, "ks", "q_raw")
         nc.vector.tensor_copy(ks[:], ks_pool[:].indirect(offsets[:]))
 
-        def spread_turns(column, name, first_bank):
+        def spread(rows, name, staged_bank, first_bank):
+            turned = psum.tile([P, P], F32, name="%s_turned" % name, tag=staged_bank)
+            nc.tensor.transpose(turned[:], rows[:], ident[:])
+            columns = sb([P, PER_ROW], F32, "%s_columns" % name)
+            nc.scalar.copy(columns[:], turned[:, 0:PER_ROW])
             banks = []
-            for half in range(PER_ROW // PACK):
-                bank = psum.tile([P, PACK, P], F32, name="%s_ps%d" % (name, half), tag="bank%d" % (first_bank + half))
+            for g in range(PASSES):
+                bank = psum.tile([P, KP], F32, name="%s_ps%d" % (name, g), tag="bank%d" % (first_bank + g))
                 for c in range(PACK):
-                    k = half * PACK + c
-                    nc.tensor.transpose(bank[:, c, :], column[:, k : k + 1].to_broadcast([P, P]), ident[:])
+                    k = g * PACK + c
+                    nc.tensor.transpose(
+                        bank[:, c * P : (c + 1) * P], columns[:, k : k + 1].to_broadcast([P, P]), ident[:]
+                    )
                 banks.append(bank)
             return banks
 
-        def spread_copies(banks, rows):
-            for g in range(len(rows)):
-                for half, bank in enumerate(banks):
-                    nc.scalar.copy(
-                        rows[g][:].rearrange("p (n c) -> p n c", c=PER_ROW)[:, :, half * PACK : (half + 1) * PACK],
-                        bank[:, :, g * P // PASSES : (g + 1) * P // PASSES].rearrange("p c n -> p n c"),
-                    )
-            return rows
+        vsc_ps = spread(staged[0], "vsc", "bank2", 0)
+        vsc_row = [placed([P, KP], F32, "vsc_row%d" % g, ROW_AT[g]) for g in range(PASSES)]
+        for g in range(PASSES):
+            nc.scalar.copy(vsc_row[g][:], vsc_ps[g][:])
+        vsc_once = sb([P, KP], F32, "vsc_once")
+        nc.scalar.copy(vsc_once[:], vsc_row[0][:])
 
-        vsc_banks = spread_turns(vsc_col, "vsc", 0)
-
-        vsc_row = spread_copies(
-            vsc_banks, [placed([P, KP], F32, "vsc_row%d" % g, ROW_AT[g]) for g in range(PASSES)]
-        )
-
-        vsc_once = spread_copies(vsc_banks, [sb([P, KP], F32, "vsc_once")])[0]
         v_codes = {}
         v_scales = {}
 
@@ -164,19 +162,13 @@ def tile_attend_beamcache_kernel(tc, query, keys_words, keys_scales, mask, size,
 
         s_sb = sb([P, I], F32, "s_sb")
         for g in range(PASSES):
-            bank = psum.tile([P, KP], F32, name="score_ps%d" % g, tag="bank%d" % (4 + g))
+            bank = psum.tile([P, KP], F32, name="score_ps%d" % g, tag="bank%d" % g)
             nc.tensor.matmul_mx(
                 out=bank[:], lhsT=q_codes[:].bitcast(FP8X4), lhsT_scale=q_scales[:],
                 rhs=kw[:, cols(g)].bitcast(FP8X4), rhs_scale=ks[:, cols(g)], start=True, stop=True,
             )
             nc.vector.tensor_tensor(s_sb[:, cols(g)], bank[:], mask_sb[:, cols(g)], ALU.add)
-        size_ps = []
-        for g in range(PASSES):
-            bank = psum.tile([P, PACK, P], F32, name="size_ps%d" % g, tag="bank%d" % (4 + g))
-            for t in range(PACK):
-                nc.tensor.transpose(bank[:, t, :], size_col[:, g, t : t + 1].to_broadcast([P, P]), ident[:])
-            size_ps.append(bank)
-
+        size_ps = spread(staged[1], "size", "bank0", 0)
         neg_max = sb([P, 1], F32, "neg_max")
         nc.vector.tensor_reduce(neg_max[:], s_sb[:], AX.X, ALU.max, negate=True)
         p_sb = sb([P, I], F32, "p_sb")
@@ -199,7 +191,7 @@ def tile_attend_beamcache_kernel(tc, query, keys_words, keys_scales, mask, size,
             gather(2, g, scaled2[:, cols(g)])
             pairs2.append(round_to_pairs(2, g, scaled2[:, cols(g)], nc.scalar.copy))
         woven1 = placed([P, PASSES, P, 2], F32, "woven1", V_AT[2])
-        turn_block(1, pairs1, "bank0", woven1)
+        turn_block(1, pairs1, "bank4", woven1)
         woven2 = sb([P, PASSES, P, 2], F32, "woven2")
         turn_block(2, pairs2, "bank3", woven2)
 
@@ -207,11 +199,7 @@ def tile_attend_beamcache_kernel(tc, query, keys_words, keys_scales, mask, size,
         w_bf = sb([P, I], BF16, "w_bf", "vsc_once")
         for g in range(PASSES):
             nc.vector.scalar_tensor_tensor(
-                w_bf[:, cols(g)].rearrange("q (n t) -> q n t", t=PACK),
-                p_sb[:, cols(g)].rearrange("q (n t) -> q n t", t=PACK),
-                inv_sum[:],
-                size_ps[g][:].rearrange("q t n -> q n t"),
-                ALU.mult, ALU.mult,
+                w_bf[:, cols(g)], p_sb[:, cols(g)], inv_sum[:], size_ps[g][:], ALU.mult, ALU.mult
             )
             words = w_bf[:, cols(g)].bitcast(F32)
             for u in range(2):
@@ -240,7 +228,7 @@ def tile_attend_beamcache_kernel(tc, query, keys_words, keys_scales, mask, size,
             quantize_values(LAST, g, woven_last[g], late_codes[:, 2, g * P : (g + 1) * P])
 
         for first, end, tag, copy in (
-            (0, 2, "bank1", nc.scalar.copy),
+            (0, 2, "bank5", nc.scalar.copy),
             (2, LAST, "bank4", nc.scalar.copy),
             (LAST, BLOCKS, "bank0", nc.vector.tensor_copy),
         ):

@@ -25,9 +25,10 @@ BLOCKS = E // P
 LAST = BLOCKS - 1
 STRIPE = 16
 QUADRANT = 32
-PER_ROW = I // P
-V_AT = (0, 8192, 16384)
-ROW_AT = (24576, 30720)
+ROWS = I // P
+ROW0 = 8
+POOL_BYTES = 4 * T
+HALF_ROW = 4 * KP
 
 
 def tile_attend_beamcache_kernel(tc, query, keys_words, keys_scales, mask, size, vsc, vals, offs, out):
@@ -35,11 +36,10 @@ def tile_attend_beamcache_kernel(tc, query, keys_words, keys_scales, mask, size,
     with ExitStack() as ctx:
         keep = ctx.enter_context(tc.tile_pool(name="keep", bufs=1))
         psum = ctx.enter_context(tc.psum_pool(name="psum", bufs=1))
+        pools = ctx.enter_context(tc.tile_pool(name="pools", bufs=1))
 
-        shared = ctx.enter_context(tc.tile_pool(name="shared", bufs=1))
-
-        def placed(shape, dtype, name, offset):
-            return shared.tile(shape, dtype, name=name, offset=offset, align_bytes=64)
+        def in_pool(b, at, shape, dtype, name):
+            return pools.tile(shape, dtype, name=name, offset=b * POOL_BYTES + at, align_bytes=64)
 
         def sb(shape, dtype, name, tag=None):
             return keep.tile(shape, dtype, name=name, tag=tag or name, align_bytes=64)
@@ -48,10 +48,11 @@ def tile_attend_beamcache_kernel(tc, query, keys_words, keys_scales, mask, size,
         nc.sync.dma_start(offsets[:], offs)
         kw_pool = sb([P, T], I32, "kw_pool")
         nc.sync.dma_start(kw_pool[:], keys_words[0].rearrange("p n t -> p (n t)").bitcast(I32))
-        staged = [sb([P, P], F32, "staged%d" % k) for k in range(2)]
-        nc.vector.memset(staged[0][:], 0.0)
-        nc.gpsimd.memset(staged[1][:], 0.0)
-        nc.sync.dma_start(staged[0][0:PER_ROW, :], vsc.rearrange("(c n) o -> c (n o)", n=P))
+        vsc_rows = sb([P, P], F32, "vsc_rows")
+        size_rows = sb([P, P], F32, "size_rows", "p_sb")
+        nc.vector.memset(vsc_rows[:], 0.0)
+        nc.gpsimd.memset(size_rows[:], 0.0)
+        nc.sync.dma_start(vsc_rows[ROW0 : ROW0 + ROWS, :], vsc.rearrange("(c n) o -> c (n o)", n=P))
         q_raw = sb([P, PACK, Q], F32, "q_raw")
         nc.sync.dma_start(q_raw[:], query.rearrange("(p t) q -> p t q", t=PACK))
         ks_pool = sb([P, T], U8, "ks_pool")
@@ -60,14 +61,18 @@ def tile_attend_beamcache_kernel(tc, query, keys_words, keys_scales, mask, size,
             nc.sync.dma_start(
                 ks_pool[r:P:QUADRANT, :].bitcast(I32), keys_scales[0, r : KP // QUADRANT : PACK, :].bitcast(I32)
             )
-        v_pool = [placed([P, T], F32, "v_pool%d" % b, V_AT[b]) for b in range(LAST)]
-        v_pool.append(sb([P, T], F32, "v_pool%d" % LAST))
-        nc.sync.dma_start(v_pool[0][:], vals[0:P, :])
-        nc.sync.dma_start(staged[1][0:PER_ROW, :], size.rearrange("o (c n) -> (o c) n", n=P))
+        v_pool = [in_pool(b, 0, [P, T], F32, "v_pool%d" % b) for b in range(BLOCKS)]
+
+        def load_values(b):
+            nc.sync.dma_start(v_pool[b][:], vals[b * P : (b + 1) * P, :])
+
+        load_values(0)
         mask_sb = sb([P, I], F32, "mask_sb")
         nc.sync.dma_start(mask_sb[:], mask)
-        for b in range(1, BLOCKS):
-            nc.sync.dma_start(v_pool[b][:], vals[b * P : (b + 1) * P, :])
+        load_values(1)
+        nc.sync.dma_start(size_rows[ROW0 : ROW0 + ROWS, :], size.rearrange("o (c n) -> (o c) n", n=P))
+        load_values(2)
+        load_values(LAST)
 
         ident = keep.tile([P, P], F32, name="ident")
         make_identity(nc, ident[:])
@@ -77,6 +82,9 @@ def tile_attend_beamcache_kernel(tc, query, keys_words, keys_scales, mask, size,
 
         def listed(g):
             return offsets[:, g * KP // STRIPE : (g + 1) * KP // STRIPE]
+
+        def as_pairs(row):
+            return row.rearrange("e (n u h) -> e u n h", u=2, h=2)
 
         kw = sb([P, I], U32, "kw")
         nc.vector.tensor_copy(kw[:], kw_pool[:].bitcast(U32).indirect(offsets[:]))
@@ -90,11 +98,11 @@ def tile_attend_beamcache_kernel(tc, query, keys_words, keys_scales, mask, size,
         ks = sb([P, I], U8, "ks", "q_raw")
         nc.vector.tensor_copy(ks[:], ks_pool[:].indirect(offsets[:]))
 
-        def spread(rows, name, staged_bank, first_bank):
-            turned = psum.tile([P, P], F32, name="%s_turned" % name, tag=staged_bank)
+        def spread(rows, name, first_bank):
+            turned = psum.tile([P, P], F32, name="%s_turned" % name, tag="bank4")
             nc.tensor.transpose(turned[:], rows[:], ident[:])
-            columns = sb([P, PER_ROW], F32, "%s_columns" % name)
-            nc.scalar.copy(columns[:], turned[:, 0:PER_ROW])
+            columns = sb([P, ROWS], F32, "%s_columns" % name)
+            nc.scalar.copy(columns[:], turned[:, ROW0 : ROW0 + ROWS])
             banks = []
             for g in range(PASSES):
                 bank = psum.tile([P, KP], F32, name="%s_ps%d" % (name, g), tag="bank%d" % (first_bank + g))
@@ -106,39 +114,38 @@ def tile_attend_beamcache_kernel(tc, query, keys_words, keys_scales, mask, size,
                 banks.append(bank)
             return banks
 
-        vsc_ps = spread(staged[0], "vsc", "bank2", 0)
-        vsc_row = [placed([P, KP], F32, "vsc_row%d" % g, ROW_AT[g]) for g in range(PASSES)]
+        vsc_ps = spread(vsc_rows, "vsc", 2)
+        vsc_sb = [sb([P, KP], F32, "vsc_sb%d" % g) for g in range(PASSES)]
         for g in range(PASSES):
-            nc.scalar.copy(vsc_row[g][:], vsc_ps[g][:])
-        vsc_once = sb([P, KP], F32, "vsc_once")
-        nc.scalar.copy(vsc_once[:], vsc_row[0][:])
+            nc.scalar.copy(vsc_sb[g][:], vsc_ps[g][:])
 
         v_codes = {}
         v_scales = {}
 
-        def gather(b, g, scaled):
-            vsc_here = vsc_once if (b, g) == (2, 0) else vsc_row[g]
-            nc.vector.tensor_tensor(scaled, v_pool[b][:].indirect(listed(g)), vsc_here[:], ALU.mult)
+        def gather_scaled(b, g, scaled):
+            nc.vector.tensor_tensor(scaled, v_pool[b][:].indirect(listed(g)), vsc_sb[g][:], ALU.mult)
 
-        def round_to_pairs(b, g, scaled, copy):
-            pairs = sb([P, 2, P, 2], BF16, "pairs%d%d" % (b, g))
-            copy(pairs[:], scaled.rearrange("e (n u h) -> e u n h", u=2, h=2))
-            return pairs
+        def gather_plain(b, g, picked):
+            nc.scalar.activation(picked, v_pool[b][:].indirect(listed(g)), ACT.Copy)
 
-        def turn_pairs(b, g, pairs, bank_tag, woven):
+        def new_pairs(b, g):
+            return sb([P, 2, P, 2], BF16, "pairs%d%d" % (b, g))
+
+        def scale_to_pairs(g, picked, pairs):
+            nc.vector.tensor_tensor(pairs[:], as_pairs(picked), as_pairs(vsc_ps[g][:]), ALU.mult)
+
+        def turn_pairs(pairs, bank):
             words = pairs[:].rearrange("e u n h -> e (u n h)").bitcast(F32)
-            bank = psum.tile([P, 2, P], F32, name="turned%d%d" % (b, g), tag=bank_tag)
             for u in range(2):
                 nc.tensor.transpose(bank[:, u, :], words[:, u * P : (u + 1) * P], ident[:])
-            nc.scalar.copy(woven, bank[:].rearrange("p u e -> p e u"))
 
-        def turn_block(b, pairs, bank_tag, woven):
-            bank = psum.tile([P, PASSES, 2, P], F32, name="turned%d" % b, tag=bank_tag)
-            for g in range(PASSES):
-                words = pairs[g][:].rearrange("e u n h -> e (u n h)").bitcast(F32)
-                for u in range(2):
-                    nc.tensor.transpose(bank[:, g, u, :], words[:, u * P : (u + 1) * P], ident[:])
-            nc.scalar.copy(woven[:], bank[:].rearrange("p g u e -> p g e u"))
+        def turn_row(row, bank):
+            words = row.bitcast(F32)
+            for u in range(2):
+                nc.tensor.transpose(bank[:, u, :], words[:, u : KP // 2 : 2], ident[:])
+
+        def weave(woven, bank):
+            nc.scalar.copy(woven, bank.rearrange("p g u e -> p g e u"))
 
         def quantize_values(b, first, woven, codes):
             count = woven.shape[1]
@@ -152,15 +159,17 @@ def tile_attend_beamcache_kernel(tc, query, keys_words, keys_scales, mask, size,
                 v_scales[b, first + k] = scales[:, k * P : (k + 1) * P]
 
         scaled0 = sb([P, I], F32, "scaled0")
-        pairs0 = []
+        pairs0 = [new_pairs(0, g) for g in range(PASSES)]
         for g in range(PASSES):
-            gather(0, g, scaled0[:, cols(g)])
-            pairs0.append(round_to_pairs(0, g, scaled0[:, cols(g)], nc.scalar.copy))
-        woven0 = placed([P, PASSES, P, 2], F32, "woven0", V_AT[0])
+            gather_scaled(0, g, scaled0[:, cols(g)])
+            nc.scalar.copy(pairs0[g][:], as_pairs(scaled0[:, cols(g)]))
+        woven0 = in_pool(0, 0, [P, PASSES, P, 2], F32, "woven0")
         for g in range(PASSES):
-            turn_pairs(0, g, pairs0[g], "bank%d" % (6 + g), woven0[:, g])
+            bank = psum.tile([P, 1, 2, P], F32, name="turned0%d" % g, tag="bank%d" % (6 + g))
+            turn_pairs(pairs0[g], bank[:, 0])
+            weave(woven0[:, g : g + 1], bank[:])
 
-        s_sb = sb([P, I], F32, "s_sb")
+        s_sb = in_pool(BLOCKS, 0, [P, I], F32, "s_sb")
         for g in range(PASSES):
             bank = psum.tile([P, KP], F32, name="score_ps%d" % g, tag="bank%d" % g)
             nc.tensor.matmul_mx(
@@ -168,80 +177,98 @@ def tile_attend_beamcache_kernel(tc, query, keys_words, keys_scales, mask, size,
                 rhs=kw[:, cols(g)].bitcast(FP8X4), rhs_scale=ks[:, cols(g)], start=True, stop=True,
             )
             nc.vector.tensor_tensor(s_sb[:, cols(g)], bank[:], mask_sb[:, cols(g)], ALU.add)
-        size_ps = spread(staged[1], "size", "bank0", 0)
         neg_max = sb([P, 1], F32, "neg_max")
         nc.vector.tensor_reduce(neg_max[:], s_sb[:], AX.X, ALU.max, negate=True)
+        block1 = sb([P, I], F32, "block1", "mask_sb")
+        gather_plain(1, 0, block1[:, cols(0)])
+        size_ps = spread(size_rows, "size", 0)
         p_sb = sb([P, I], F32, "p_sb")
         row_sum = sb([P, 1], F32, "row_sum")
         nc.scalar.activation(p_sb[:], s_sb[:], ACT.Exp, bias=neg_max[:], accum_out=row_sum[:])
 
-
-        scaled1 = sb([P, I], F32, "scaled1", "mask_sb")
-        pairs1 = []
-        for g in range(PASSES):
-            gather(1, g, scaled1[:, cols(g)])
-            pairs1.append(round_to_pairs(1, g, scaled1[:, cols(g)], nc.scalar.copy))
-        quantize_values(0, 0, woven0, placed([P, PASSES * P], U32, "codes0", V_AT[1] + 4096)[:])
-        inv_sum = placed([P, 1], F32, "inv_sum", V_AT[1] + 2048)
+        gather_scaled(1, 1, block1[:, cols(1)])
+        pairs10 = new_pairs(1, 0)
+        scale_to_pairs(0, block1[:, cols(0)], pairs10)
+        rounded11 = sb([P, KP], BF16, "rounded11")
+        nc.gpsimd.tensor_scalar(rounded11[:], block1[:, cols(1)], 1.0, 0.0, ALU.mult, ALU.add)
+        turned1 = psum.tile([P, PASSES, 2, P], F32, name="turned1", tag="bank4")
+        turn_pairs(pairs10, turned1[:, 0])
+        turn_row(rounded11[:], turned1[:, 1])
+        inv_sum = sb([P, 1], F32, "inv_sum")
         nc.vector.reciprocal(inv_sum[:], row_sum[:])
+        quantize_values(0, 0, woven0, in_pool(BLOCKS, 0, [P, PASSES * P], U32, "codes0")[:])
 
-        pairs2 = []
-        scaled2 = sb([P, I], F32, "scaled2", "s_sb")
+        block2 = sb([P, I], F32, "block2")
         for g in range(PASSES):
-            gather(2, g, scaled2[:, cols(g)])
-            pairs2.append(round_to_pairs(2, g, scaled2[:, cols(g)], nc.scalar.copy))
-        woven1 = placed([P, PASSES, P, 2], F32, "woven1", V_AT[2])
-        turn_block(1, pairs1, "bank4", woven1)
-        woven2 = sb([P, PASSES, P, 2], F32, "woven2")
-        turn_block(2, pairs2, "bank3", woven2)
+            gather_plain(2, g, block2[:, cols(g)])
+        woven1 = in_pool(2, 0, [P, PASSES, P, 2], F32, "woven1")
+        weave(woven1[:], turned1[:])
+        rounded20 = in_pool(0, 0, [P, KP], BF16, "rounded20")
+        nc.gpsimd.tensor_tensor(rounded20[:], block2[:, cols(0)], vsc_sb[0][:], ALU.mult)
 
         w_ps = psum.tile([P, PASSES, 2, Q], F32, name="w_ps", tag="bank2")
-        w_bf = sb([P, I], BF16, "w_bf", "vsc_once")
-        for g in range(PASSES):
+        w_bf = sb([P, I], BF16, "w_bf")
+        wt = [in_pool(2 + g, 2048, [P, 1, Q, 2], F32, "wt%d" % g) for g in range(PASSES)]
+
+        def weigh(g):
             nc.vector.scalar_tensor_tensor(
                 w_bf[:, cols(g)], p_sb[:, cols(g)], inv_sum[:], size_ps[g][:], ALU.mult, ALU.mult
             )
-            words = w_bf[:, cols(g)].bitcast(F32)
-            for u in range(2):
-                nc.tensor.transpose(w_ps[:, g, u, :], words[:, u : KP // 2 : 2], ident[:])
-        wt = sb([P, PASSES, Q, 2], F32, "wt")
-        nc.scalar.copy(wt[:], w_ps[:].rearrange("p g u q -> p g q u"))
+            turn_row(w_bf[:, cols(g)], w_ps[:, g])
 
-        scaled3 = placed([P, I], F32, "scaled3", V_AT[2] + 4096)
+        weigh(0)
+        weave(wt[0][:], w_ps[:, 0:1])
+        weigh(1)
+        pairs21 = new_pairs(2, 1)
+        scale_to_pairs(1, block2[:, cols(1)], pairs21)
+        turned2 = psum.tile([P, PASSES, 2, P], F32, name="turned2", tag="bank5")
+        turn_row(rounded20[:], turned2[:, 0])
+        turn_pairs(pairs21, turned2[:, 1])
+
+        scaled30 = sb([P, KP], F32, "scaled30")
+        gather_scaled(LAST, 0, scaled30[:])
+        picked31 = in_pool(BLOCKS, 4096, [P, KP], F32, "picked31")
+        gather_plain(LAST, 1, picked31[:])
+        weave(wt[1][:], w_ps[:, 1:2])
+        woven2 = in_pool(LAST, 0, [P, PASSES, P, 2], F32, "woven2")
+        weave(woven2[:], turned2[:])
+        pairs3 = [in_pool(LAST, 4096, [P, 2, P, 2], BF16, "pairs30"), new_pairs(LAST, 1)]
+        scale_to_pairs(1, picked31[:], pairs3[1])
+        nc.vector.tensor_copy(pairs3[0][:], as_pairs(scaled30[:]))
+        woven3 = [sb([P, 1, P, 2], F32, "woven3%d" % g) for g in range(PASSES)]
+        for g in reversed(range(PASSES)):
+            bank = psum.tile([P, 1, 2, P], F32, name="turned3%d" % g, tag="bank%d" % (6 + g))
+            turn_pairs(pairs3[g], bank[:, 0])
+            weave(woven3[g][:], bank[:])
+
+        quantize_values(1, 0, woven1, sb([P, PASSES * P], U32, "codes1")[:])
+        w_codes = [sb([P, Q], U32, "w_codes0"), in_pool(BLOCKS, 4096, [P, Q], U32, "w_codes1")]
+        w_scales = [sb([P, Q], U8, "w_scales%d" % g) for g in range(PASSES)]
         for g in range(PASSES):
-            gather(LAST, g, scaled3[:, cols(g)])
-        woven_last = [sb([P, 1, P, 2], F32, "woven_last%d" % g) for g in range(PASSES)]
-        for g in range(PASSES):
-            pairs = placed([P, 2, P, 2], BF16, "pairs3%d" % g, ROW_AT[0] + 1024 * g)
-            nc.vector.tensor_copy(pairs[:], scaled3[:, cols(g)].rearrange("e (n u h) -> e u n h", u=2, h=2))
-            turn_pairs(LAST, g, pairs, "bank%d" % (6 + g), woven_last[g][:, 0])
-        w_codes = placed([P, PASSES * Q], U32, "w_codes", ROW_AT[1] + 1024)
-        w_scales = sb([P, PASSES * Q], U8, "w_scales")
-        nc.vector.quantize_mx(
-            out=w_codes[:].bitcast(FP8X4), scales=w_scales[:],
-            in_=wt[:].rearrange("p g q u -> p (g q u)").bitcast(BF16),
-        )
-        late_codes = placed([P, LAST, PASSES * P], U32, "late_codes", ROW_AT[1] + 64 - 3072)
-        quantize_values(1, 0, woven1, late_codes[:, 0, :])
-        quantize_values(2, 0, woven2, late_codes[:, 1, :])
-        for g in range(PASSES):
-            quantize_values(LAST, g, woven_last[g], late_codes[:, 2, g * P : (g + 1) * P])
+            nc.vector.quantize_mx(
+                out=w_codes[g][:].bitcast(FP8X4), scales=w_scales[g][:],
+                in_=wt[g][:].rearrange("p g q u -> p (g q u)").bitcast(BF16),
+            )
+        quantize_values(2, 0, woven2, sb([P, PASSES * P], U32, "codes2")[:])
+        for g in reversed(range(PASSES)):
+            quantize_values(LAST, g, woven3[g], sb([P, P], U32, "codes3%d" % g)[:])
+
 
         for first, end, tag, copy in (
-            (0, 2, "bank5", nc.scalar.copy),
-            (2, LAST, "bank4", nc.scalar.copy),
-            (LAST, BLOCKS, "bank0", nc.vector.tensor_copy),
+            (0, 2, "bank0", nc.scalar.copy),
+            (2, LAST, "bank1", nc.scalar.copy),
+            (LAST, BLOCKS, "bank3", nc.vector.tensor_copy),
         ):
             acc = psum.tile([P, (end - first) * P], F32, name="acc%d" % first, tag=tag)
-            for b in range(first, end):
-                for g in range(PASSES):
-                    rows = slice(g * Q, (g + 1) * Q)
-                    nc.tensor.matmul_mx(
-                        out=acc[:, (b - first) * P : (b - first + 1) * P],
-                        lhsT=w_codes[:, rows].bitcast(FP8X4), lhsT_scale=w_scales[:, rows],
-                        rhs=v_codes[b, g].bitcast(FP8X4), rhs_scale=v_scales[b, g],
-                        start=(g == 0), stop=(g == PASSES - 1),
-                    )
+            order = reversed(range(PASSES)) if first == LAST else range(PASSES)
+            steps = [(b, g) for g in order for b in range(first, end)]
+            for b, g in steps:
+                nc.tensor.matmul_mx(
+                    out=acc[:, (b - first) * P : (b - first + 1) * P],
+                    lhsT=w_codes[g][:].bitcast(FP8X4), lhsT_scale=w_scales[g][:],
+                    rhs=v_codes[b, g].bitcast(FP8X4), rhs_scale=v_scales[b, g],
+                    start=((b, g) == steps[0]), stop=((b, g) == steps[-1]),
+                )
             result = sb([P, (end - first) * P], F32, "result%d" % first)
             copy(result[:], acc[:])
             nc.sync.dma_start(out[:, first * P : end * P], result[:])

@@ -29,6 +29,9 @@ ROWS = I // P
 ROW0 = 8
 POOL_BYTES = 4 * T
 HALF_ROW = 4 * KP
+VSC_AT = 512
+PIECE = KP // 2
+SCORE_BANKS = (0, 1, 5, 6)
 
 
 def tile_attend_beamcache_kernel(tc, query, keys_words, keys_scales, mask, size, vsc, vals, offs, out):
@@ -46,33 +49,31 @@ def tile_attend_beamcache_kernel(tc, query, keys_words, keys_scales, mask, size,
 
         offsets = keep.tile([P, I // STRIPE], U16, name="offsets")
         nc.sync.dma_start(offsets[:], offs)
-        kw_pool = sb([P, T], I32, "kw_pool")
-        nc.sync.dma_start(kw_pool[:], keys_words[0].rearrange("p n t -> p (n t)").bitcast(I32))
-        vsc_rows = sb([P, P], F32, "vsc_rows")
-        size_rows = sb([P, P], F32, "size_rows", "p_sb")
-        nc.vector.memset(vsc_rows[:], 0.0)
-        nc.gpsimd.memset(size_rows[:], 0.0)
-        nc.sync.dma_start(vsc_rows[ROW0 : ROW0 + ROWS, :], vsc.rearrange("(c n) o -> c (n o)", n=P))
-        q_raw = sb([P, PACK, Q], F32, "q_raw")
-        nc.sync.dma_start(q_raw[:], query.rearrange("(p t) q -> p t q", t=PACK))
         ks_pool = sb([P, T], U8, "ks_pool")
         nc.vector.memset(ks_pool[:].bitcast(I32), 0)
+        size_rows = sb([P, P], F32, "size_rows", "p_sb")
+        nc.gpsimd.memset(size_rows[:], 0.0)
+        vsc_columns = sb([P, PASSES, 2 * PACK], F32, "vsc_columns")
+        nc.sync.dma_start(vsc_columns[:, :, 0:PACK], vsc.rearrange("(g p t) o -> p g (t o)", g=PASSES, t=PACK))
+        q_raw = sb([P, PACK, Q], F32, "q_raw")
+        nc.sync.dma_start(q_raw[:], query.rearrange("(p t) q -> p t q", t=PACK))
         for r in range(PACK):
             nc.sync.dma_start(
                 ks_pool[r:P:QUADRANT, :].bitcast(I32), keys_scales[0, r : KP // QUADRANT : PACK, :].bitcast(I32)
             )
+        kw_pool = sb([P, T], I32, "kw_pool")
+        nc.sync.dma_start(kw_pool[:], keys_words[0].rearrange("p n t -> p (n t)").bitcast(I32))
         v_pool = [in_pool(b, 0, [P, T], F32, "v_pool%d" % b) for b in range(BLOCKS)]
 
         def load_values(b):
             nc.sync.dma_start(v_pool[b][:], vals[b * P : (b + 1) * P, :])
 
-        load_values(0)
         mask_sb = sb([P, I], F32, "mask_sb")
         nc.sync.dma_start(mask_sb[:], mask)
-        load_values(1)
+        load_values(0)
         nc.sync.dma_start(size_rows[ROW0 : ROW0 + ROWS, :], size.rearrange("o (c n) -> (o c) n", n=P))
-        load_values(2)
-        load_values(LAST)
+        for b in range(1, BLOCKS):
+            load_values(b)
 
         ident = keep.tile([P, P], F32, name="ident")
         make_identity(nc, ident[:])
@@ -83,11 +84,15 @@ def tile_attend_beamcache_kernel(tc, query, keys_words, keys_scales, mask, size,
         def listed(g):
             return offsets[:, g * KP // STRIPE : (g + 1) * KP // STRIPE]
 
+        def piece(k):
+            return slice(k * PIECE, (k + 1) * PIECE)
+
+        def piece_listed(k):
+            return offsets[:, k * PIECE // STRIPE : (k + 1) * PIECE // STRIPE]
+
         def as_pairs(row):
             return row.rearrange("e (n u h) -> e u n h", u=2, h=2)
 
-        kw = sb([P, I], U32, "kw")
-        nc.vector.tensor_copy(kw[:], kw_pool[:].bitcast(U32).indirect(offsets[:]))
         q_bf = sb([P, Q, PACK], BF16, "q_bf")
         nc.scalar.copy(q_bf[:], q_raw[:].rearrange("p t q -> p q t"))
         q_codes = sb([P, Q], U32, "q_codes")
@@ -95,8 +100,11 @@ def tile_attend_beamcache_kernel(tc, query, keys_words, keys_scales, mask, size,
         nc.vector.quantize_mx(
             out=q_codes[:].bitcast(FP8X4), scales=q_scales[:], in_=q_bf[:].rearrange("p q t -> p (q t)")
         )
-        ks = sb([P, I], U8, "ks", "q_raw")
+        ks = sb([P, I], U8, "ks")
         nc.vector.tensor_copy(ks[:], ks_pool[:].indirect(offsets[:]))
+        kw = [sb([P, PIECE], U32, "kw%d" % k) for k in range(I // PIECE)]
+        for k in range(I // PIECE):
+            nc.vector.tensor_copy(kw[k][:], kw_pool[:].bitcast(U32).indirect(piece_listed(k)))
 
         def spread(rows, name, first_bank):
             turned = psum.tile([P, P], F32, name="%s_turned" % name, tag="bank4")
@@ -114,10 +122,22 @@ def tile_attend_beamcache_kernel(tc, query, keys_words, keys_scales, mask, size,
                 banks.append(bank)
             return banks
 
-        vsc_ps = spread(vsc_rows, "vsc", 2)
-        vsc_sb = [sb([P, KP], F32, "vsc_sb%d" % g) for g in range(PASSES)]
+        vsc_ps = []
         for g in range(PASSES):
-            nc.scalar.copy(vsc_sb[g][:], vsc_ps[g][:])
+            bank = psum.tile([P, PACK, P], F32, name="vsc_ps%d" % g, tag="bank%d" % (2 + g))
+            for t in range(PACK):
+                nc.tensor.transpose(bank[:, t, :], vsc_columns[:, g, t : t + 1].to_broadcast([P, P]), ident[:])
+            vsc_ps.append(bank)
+        vsc_sb = [in_pool(BLOCKS, VSC_AT + g * 2 * HALF_ROW, [P, KP], F32, "vsc_sb%d" % g) for g in range(PASSES)]
+        for g in range(PASSES):
+            nc.scalar.copy(vsc_sb[g][:].rearrange("e (n t) -> e n t", t=PACK), vsc_ps[g][:].rearrange("e t n -> e n t"))
+
+        vsc_tail = sb([P, PASSES, PIECE], F32, "vsc_tail")
+        for g in range(PASSES):
+            nc.scalar.copy(
+                vsc_tail[:, g].rearrange("e (n t) -> e n t", t=PACK),
+                vsc_ps[g][:, :, 0 : P // 2].rearrange("e t n -> e n t"),
+            )
 
         v_codes = {}
         v_scales = {}
@@ -132,7 +152,7 @@ def tile_attend_beamcache_kernel(tc, query, keys_words, keys_scales, mask, size,
             return sb([P, 2, P, 2], BF16, "pairs%d%d" % (b, g))
 
         def scale_to_pairs(g, picked, pairs):
-            nc.vector.tensor_tensor(pairs[:], as_pairs(picked), as_pairs(vsc_ps[g][:]), ALU.mult)
+            nc.vector.tensor_tensor(pairs[:], as_pairs(picked), vsc_ps[g][:].rearrange("e (u h) n -> e u n h", h=2), ALU.mult)
 
         def turn_pairs(pairs, bank):
             words = pairs[:].rearrange("e u n h -> e (u n h)").bitcast(F32)
@@ -158,117 +178,132 @@ def tile_attend_beamcache_kernel(tc, query, keys_words, keys_scales, mask, size,
                 v_codes[b, first + k] = codes[:, k * P : (k + 1) * P]
                 v_scales[b, first + k] = scales[:, k * P : (k + 1) * P]
 
-        scaled0 = sb([P, I], F32, "scaled0")
-        pairs0 = [new_pairs(0, g) for g in range(PASSES)]
-        for g in range(PASSES):
-            gather_scaled(0, g, scaled0[:, cols(g)])
-            nc.scalar.copy(pairs0[g][:], as_pairs(scaled0[:, cols(g)]))
-        woven0 = in_pool(0, 0, [P, PASSES, P, 2], F32, "woven0")
-        for g in range(PASSES):
-            bank = psum.tile([P, 1, 2, P], F32, name="turned0%d" % g, tag="bank%d" % (6 + g))
-            turn_pairs(pairs0[g], bank[:, 0])
-            weave(woven0[:, g : g + 1], bank[:])
+        def round_row(rounded, scaled):
+            nc.gpsimd.tensor_scalar(rounded, scaled, 1.0, 0.0, ALU.mult, ALU.add)
 
-        s_sb = in_pool(BLOCKS, 0, [P, I], F32, "s_sb")
-        for g in range(PASSES):
-            bank = psum.tile([P, KP], F32, name="score_ps%d" % g, tag="bank%d" % g)
+        def row(name, dtype=F32):
+            return sb([P, KP], dtype, name)
+
+        s_sb = sb([P, I], F32, "s_sb")
+        for k, tag in enumerate(SCORE_BANKS):
+            bank = psum.tile([P, PIECE], F32, name="score_ps%d" % k, tag="bank%d" % tag)
             nc.tensor.matmul_mx(
                 out=bank[:], lhsT=q_codes[:].bitcast(FP8X4), lhsT_scale=q_scales[:],
-                rhs=kw[:, cols(g)].bitcast(FP8X4), rhs_scale=ks[:, cols(g)], start=True, stop=True,
+                rhs=kw[k][:].bitcast(FP8X4), rhs_scale=ks[:, piece(k)], start=True, stop=True,
             )
-            nc.vector.tensor_tensor(s_sb[:, cols(g)], bank[:], mask_sb[:, cols(g)], ALU.add)
+            nc.vector.tensor_tensor(s_sb[:, piece(k)], bank[:], mask_sb[:, piece(k)], ALU.add)
         neg_max = sb([P, 1], F32, "neg_max")
         nc.vector.tensor_reduce(neg_max[:], s_sb[:], AX.X, ALU.max, negate=True)
-        block1 = sb([P, I], F32, "block1", "mask_sb")
-        gather_plain(1, 0, block1[:, cols(0)])
+
+        picked00 = row("picked00")
+        gather_plain(0, 0, picked00[:])
         size_ps = spread(size_rows, "size", 0)
         p_sb = sb([P, I], F32, "p_sb")
         row_sum = sb([P, 1], F32, "row_sum")
         nc.scalar.activation(p_sb[:], s_sb[:], ACT.Exp, bias=neg_max[:], accum_out=row_sum[:])
+        scaled01 = row("scaled01")
+        gather_scaled(0, 1, scaled01[:])
+        pairs00 = new_pairs(0, 0)
+        scale_to_pairs(0, picked00[:], pairs00)
+        rounded01 = row("rounded01", BF16)
+        round_row(rounded01[:], scaled01[:])
+        turned0 = psum.tile([P, PASSES, 2, P], F32, name="turned0", tag="bank4")
+        turn_pairs(pairs00, turned0[:, 0])
+        turn_row(rounded01[:], turned0[:, 1])
 
-        gather_scaled(1, 1, block1[:, cols(1)])
-        pairs10 = new_pairs(1, 0)
-        scale_to_pairs(0, block1[:, cols(0)], pairs10)
-        rounded11 = sb([P, KP], BF16, "rounded11")
-        nc.gpsimd.tensor_scalar(rounded11[:], block1[:, cols(1)], 1.0, 0.0, ALU.mult, ALU.add)
-        turned1 = psum.tile([P, PASSES, 2, P], F32, name="turned1", tag="bank4")
-        turn_pairs(pairs10, turned1[:, 0])
-        turn_row(rounded11[:], turned1[:, 1])
         inv_sum = sb([P, 1], F32, "inv_sum")
         nc.vector.reciprocal(inv_sum[:], row_sum[:])
-        quantize_values(0, 0, woven0, in_pool(BLOCKS, 0, [P, PASSES * P], U32, "codes0")[:])
-
-        block2 = sb([P, I], F32, "block2")
-        for g in range(PASSES):
-            gather_plain(2, g, block2[:, cols(g)])
-        woven1 = in_pool(2, 0, [P, PASSES, P, 2], F32, "woven1")
-        weave(woven1[:], turned1[:])
-        rounded20 = in_pool(0, 0, [P, KP], BF16, "rounded20")
-        nc.gpsimd.tensor_tensor(rounded20[:], block2[:, cols(0)], vsc_sb[0][:], ALU.mult)
-
-        w_ps = psum.tile([P, PASSES, 2, Q], F32, name="w_ps", tag="bank2")
         w_bf = sb([P, I], BF16, "w_bf")
-        wt = [in_pool(2 + g, 2048, [P, 1, Q, 2], F32, "wt%d" % g) for g in range(PASSES)]
-
-        def weigh(g):
+        w_ps = [psum.tile([P, 1, 2, Q], F32, name="w_ps%d" % g, tag="bank%d" % (5 + g)) for g in range(PASSES)]
+        for g in range(PASSES):
             nc.vector.scalar_tensor_tensor(
                 w_bf[:, cols(g)], p_sb[:, cols(g)], inv_sum[:], size_ps[g][:], ALU.mult, ALU.mult
             )
-            turn_row(w_bf[:, cols(g)], w_ps[:, g])
+            turn_row(w_bf[:, cols(g)], w_ps[g][:, 0])
 
-        weigh(0)
-        weave(wt[0][:], w_ps[:, 0:1])
-        weigh(1)
-        pairs21 = new_pairs(2, 1)
-        scale_to_pairs(1, block2[:, cols(1)], pairs21)
-        turned2 = psum.tile([P, PASSES, 2, P], F32, name="turned2", tag="bank5")
-        turn_row(rounded20[:], turned2[:, 0])
-        turn_pairs(pairs21, turned2[:, 1])
+        picked1 = [row("picked1%d" % g) for g in range(PASSES)]
+        for g in range(PASSES):
+            gather_plain(1, g, picked1[g][:])
+        rounded10 = row("rounded10", BF16)
+        nc.gpsimd.tensor_tensor(rounded10[:], picked1[0][:], vsc_sb[0][:], ALU.mult)
+        pairs11 = new_pairs(1, 1)
+        scale_to_pairs(1, picked1[1][:], pairs11)
+        turned1 = psum.tile([P, PASSES, 2, P], F32, name="turned1", tag="bank7")
+        turn_pairs(pairs11, turned1[:, 1])
+        turn_row(rounded10[:], turned1[:, 0])
+        woven0 = in_pool(1, 0, [P, PASSES, P, 2], F32, "woven0")
+        weave(woven0[:], turned0[:])
+        wt = [in_pool(1 + g, HALF_ROW, [P, 1, Q, 2], F32, "wt%d" % g) for g in range(PASSES)]
+        weave(wt[0][:], w_ps[0][:])
+        quantize_values(0, 0, woven0, sb([P, PASSES * P], U32, "codes0")[:])
+        w_codes = [in_pool(LAST, 4096 + g * 4 * Q, [P, Q], U32, "w_codes%d" % g) for g in range(PASSES)]
+        w_scales = [sb([P, Q], U8, "w_scales%d" % g) for g in range(PASSES)]
 
-        scaled30 = sb([P, KP], F32, "scaled30")
-        gather_scaled(LAST, 0, scaled30[:])
-        picked31 = in_pool(BLOCKS, 4096, [P, KP], F32, "picked31")
-        gather_plain(LAST, 1, picked31[:])
-        weave(wt[1][:], w_ps[:, 1:2])
+        def multiply(acc, b, order):
+            for g in order:
+                nc.tensor.matmul_mx(
+                    out=acc,
+                    lhsT=w_codes[g][:].bitcast(FP8X4), lhsT_scale=w_scales[g][:],
+                    rhs=v_codes[b, g].bitcast(FP8X4), rhs_scale=v_scales[b, g],
+                    start=(g == order[0]), stop=(g == order[-1]),
+                )
+
+        picked20 = row("picked20")
+        gather_plain(2, 0, picked20[:])
+        scaled21 = row("scaled21")
+        gather_scaled(2, 1, scaled21[:])
+        pairs20 = new_pairs(2, 0)
+        scale_to_pairs(0, picked20[:], pairs20)
+        rounded21 = row("rounded21", BF16)
+        round_row(rounded21[:], scaled21[:])
+        woven1 = in_pool(BLOCKS, VSC_AT + 2 * HALF_ROW, [P, PASSES, P, 2], F32, "woven1")
+        weave(woven1[:], turned1[:])
+        nc.vector.tensor_copy(wt[1][:], w_ps[1][:].rearrange("p g u e -> p g e u"))
+        turned2 = psum.tile([P, PASSES, 2, P], F32, name="turned2", tag="bank4")
+        turn_pairs(pairs20, turned2[:, 0])
+        turn_row(rounded21[:], turned2[:, 1])
+
+        front = [sb([P, PIECE], F32, "front3%d" % g) for g in range(PASSES)]
+        back = [sb([P, PIECE], F32, "back3%d" % g) for g in range(PASSES)]
+        rounded3 = [row("rounded3%d" % g, BF16) for g in range(PASSES)]
+        for g in range(PASSES):
+            nc.vector.tensor_tensor(
+                front[g][:], v_pool[LAST][:].indirect(piece_listed(2 * g)), vsc_tail[:, g], ALU.mult
+            )
+            nc.scalar.activation(back[g][:], v_pool[LAST][:].indirect(piece_listed(2 * g + 1)), ACT.Copy)
+        for g in range(PASSES):
+            nc.vector.tensor_tensor(
+                rounded3[g][:, piece(1)].rearrange("e (n t) -> e n t", t=PACK),
+                back[g][:].rearrange("e (n t) -> e n t", t=PACK),
+                vsc_ps[g][:, :, P // 2 :].rearrange("e t n -> e n t"),
+                ALU.mult,
+            )
+            nc.scalar.copy(rounded3[g][:, piece(0)], front[g][:])
         woven2 = in_pool(LAST, 0, [P, PASSES, P, 2], F32, "woven2")
         weave(woven2[:], turned2[:])
-        pairs3 = [in_pool(LAST, 4096, [P, 2, P, 2], BF16, "pairs30"), new_pairs(LAST, 1)]
-        scale_to_pairs(1, picked31[:], pairs3[1])
-        nc.vector.tensor_copy(pairs3[0][:], as_pairs(scaled30[:]))
         woven3 = [sb([P, 1, P, 2], F32, "woven3%d" % g) for g in range(PASSES)]
-        for g in reversed(range(PASSES)):
-            bank = psum.tile([P, 1, 2, P], F32, name="turned3%d" % g, tag="bank%d" % (6 + g))
-            turn_pairs(pairs3[g], bank[:, 0])
+        for g in range(PASSES):
+            bank = psum.tile([P, 1, 2, P], F32, name="turned3%d" % g, tag="bank%d" % g)
+            turn_row(rounded3[g][:], bank[:, 0])
             weave(woven3[g][:], bank[:])
 
-        quantize_values(1, 0, woven1, sb([P, PASSES * P], U32, "codes1")[:])
-        w_codes = [sb([P, Q], U32, "w_codes0"), in_pool(BLOCKS, 4096, [P, Q], U32, "w_codes1")]
-        w_scales = [sb([P, Q], U8, "w_scales%d" % g) for g in range(PASSES)]
         for g in range(PASSES):
             nc.vector.quantize_mx(
                 out=w_codes[g][:].bitcast(FP8X4), scales=w_scales[g][:],
                 in_=wt[g][:].rearrange("p g q u -> p (g q u)").bitcast(BF16),
             )
+        quantize_values(1, 0, woven1, in_pool(LAST, HALF_ROW, [P, PASSES * P], U32, "codes1")[:])
         quantize_values(2, 0, woven2, sb([P, PASSES * P], U32, "codes2")[:])
-        for g in reversed(range(PASSES)):
+        for g in range(PASSES):
             quantize_values(LAST, g, woven3[g], sb([P, P], U32, "codes3%d" % g)[:])
-
-
         for first, end, tag, copy in (
-            (0, 2, "bank0", nc.scalar.copy),
-            (2, LAST, "bank1", nc.scalar.copy),
-            (LAST, BLOCKS, "bank3", nc.vector.tensor_copy),
+            (0, 2, "bank5", nc.scalar.copy),
+            (2, LAST, "bank7", nc.scalar.copy),
+            (LAST, BLOCKS, "bank6", nc.vector.tensor_copy),
         ):
-            acc = psum.tile([P, (end - first) * P], F32, name="acc%d" % first, tag=tag)
-            order = reversed(range(PASSES)) if first == LAST else range(PASSES)
-            steps = [(b, g) for g in order for b in range(first, end)]
-            for b, g in steps:
-                nc.tensor.matmul_mx(
-                    out=acc[:, (b - first) * P : (b - first + 1) * P],
-                    lhsT=w_codes[g][:].bitcast(FP8X4), lhsT_scale=w_scales[g][:],
-                    rhs=v_codes[b, g].bitcast(FP8X4), rhs_scale=v_scales[b, g],
-                    start=((b, g) == steps[0]), stop=((b, g) == steps[-1]),
-                )
+            acc = psum.tile([P, end - first, P], F32, name="acc%d" % first, tag=tag)
+            for b in range(first, end):
+                multiply(acc[:, b - first], b, [0, 1])
             result = sb([P, (end - first) * P], F32, "result%d" % first)
-            copy(result[:], acc[:])
+            copy(result[:], acc[:].rearrange("p b e -> p (b e)"))
             nc.sync.dma_start(out[:, first * P : end * P], result[:])

@@ -265,7 +265,7 @@ def tile_attend_beamcache_kernel(tc, query, keys_words, keys_scales, mask, size,
 
         front = [sb([P, PIECE], F32, "front3%d" % g) for g in range(PASSES)]
         back = [sb([P, PIECE], F32, "back3%d" % g) for g in range(PASSES)]
-        rounded3 = [row("rounded3%d" % g, BF16) for g in range(PASSES)]
+        pairs3 = [new_pairs(LAST, g) for g in range(PASSES)]
         for g in range(PASSES):
             nc.vector.tensor_tensor(
                 front[g][:], v_pool[LAST][:].indirect(piece_listed(2 * g)), vsc_tail[:, g], ALU.mult
@@ -273,18 +273,18 @@ def tile_attend_beamcache_kernel(tc, query, keys_words, keys_scales, mask, size,
             nc.scalar.activation(back[g][:], v_pool[LAST][:].indirect(piece_listed(2 * g + 1)), ACT.Copy)
         for g in range(PASSES):
             nc.vector.tensor_tensor(
-                rounded3[g][:, piece(1)].rearrange("e (n t) -> e n t", t=PACK),
-                back[g][:].rearrange("e (n t) -> e n t", t=PACK),
-                vsc_ps[g][:, :, P // 2 :].rearrange("e t n -> e n t"),
+                pairs3[g][:, :, P // 2 :, :],
+                as_pairs(back[g][:]),
+                vsc_ps[g][:, :, P // 2 :].rearrange("e (u h) n -> e u n h", h=2),
                 ALU.mult,
             )
-            nc.scalar.copy(rounded3[g][:, piece(0)], front[g][:])
+            nc.scalar.copy(pairs3[g][:, :, 0 : P // 2, :], as_pairs(front[g][:]))
         woven2 = in_pool(LAST, 0, [P, PASSES, P, 2], F32, "woven2")
         weave(woven2[:], turned2[:])
         woven3 = [sb([P, 1, P, 2], F32, "woven3%d" % g) for g in range(PASSES)]
         for g in range(PASSES):
             bank = psum.tile([P, 1, 2, P], F32, name="turned3%d" % g, tag="bank%d" % g)
-            turn_row(rounded3[g][:], bank[:, 0])
+            turn_pairs(pairs3[g], bank[:, 0])
             weave(woven3[g][:], bank[:])
 
         for g in range(PASSES):

@@ -233,9 +233,11 @@ def tile_attend_beamcache_kernel(tc, query, keys_words, keys_scales, mask, size,
         turn_row(rounded10[:], turned1[:, 0])
         woven0 = in_pool(1, 0, [P, PASSES, P, 2], F32, "woven0")
         weave(woven0[:], turned0[:])
-        wt = [in_pool(1 + g, HALF_ROW, [P, 1, Q, 2], F32, "wt%d" % g) for g in range(PASSES)]
+        wt = [
+            in_pool(1, HALF_ROW, [P, 1, Q, 2], F32, "wt0"),
+            in_pool(BLOCKS, VSC_AT + 2 * HALF_ROW + 64 - 8 * Q, [P, 1, Q, 2], F32, "wt1"),
+        ]
         weave(wt[0][:], w_ps[0][:])
-        quantize_values(0, 0, woven0, sb([P, PASSES * P], U32, "codes0")[:])
         w_codes = [in_pool(LAST, 4096 + g * 4 * Q, [P, Q], U32, "w_codes%d" % g) for g in range(PASSES)]
         w_scales = [sb([P, Q], U8, "w_scales%d" % g) for g in range(PASSES)]
 
@@ -256,9 +258,10 @@ def tile_attend_beamcache_kernel(tc, query, keys_words, keys_scales, mask, size,
         scale_to_pairs(0, picked20[:], pairs20)
         rounded21 = row("rounded21", BF16)
         round_row(rounded21[:], scaled21[:])
-        woven1 = in_pool(BLOCKS, VSC_AT + 2 * HALF_ROW, [P, PASSES, P, 2], F32, "woven1")
+        woven1 = in_pool(BLOCKS, VSC_AT + 2 * HALF_ROW + 64, [P, PASSES, P, 2], F32, "woven1")
         weave(woven1[:], turned1[:])
-        nc.vector.tensor_copy(wt[1][:], w_ps[1][:].rearrange("p g u e -> p g e u"))
+        weave(wt[1][:], w_ps[1][:])
+        quantize_values(0, 0, woven0, in_pool(2, 0, [P, PASSES * P], U32, "codes0")[:])
         turned2 = psum.tile([P, PASSES, 2, P], F32, name="turned2", tag="bank4")
         turn_pairs(pairs20, turned2[:, 0])
         turn_row(rounded21[:], turned2[:, 1])

from contextlib import ExitStack

import concourse.mybir as mybir
from concourse.masks import make_identity

D, T, I, Q, E = 512, 2048, 1024, 128, 512
FLOPS = 2 * Q * I * D + 2 * Q * I * E

F32 = mybir.dt.float32
BF16 = mybir.dt.bfloat16
I32 = mybir.dt.int32
U32 = mybir.dt.uint32
U16 = mybir.dt.uint16
U8 = mybir.dt.uint8
FP8X4 = mybir.dt.float8_e4m3fn_x4
ALU = mybir.AluOpType
ACT = mybir.ActivationFunctionType
AX = mybir.AxisListType

P = 128
PACK = 4
KP = P * PACK
PASSES = I // KP
BLOCKS = E // P
LAST = BLOCKS - 1
STRIPE = 16
QUADRANT = 32
ROWS = I // P
ROW0 = 8
POOL_BYTES = 4 * T
HALF_ROW = 4 * KP
VSC_AT = 512
PIECE = KP // 2
SCORE_BANKS = (0, 1, 5, 6)


def tile_attend_beamcache_kernel(tc, query, keys_words, keys_scales, mask, size, vsc, vals, offs, out):
    nc = tc.nc
    with ExitStack() as ctx:
        keep = ctx.enter_context(tc.tile_pool(name="keep", bufs=1))
        psum = ctx.enter_context(tc.psum_pool(name="psum", bufs=1))
        pools = ctx.enter_context(tc.tile_pool(name="pools", bufs=1))

        def in_pool(b, at, shape, dtype, name):
            return pools.tile(shape, dtype, name=name, offset=b * POOL_BYTES + at, align_bytes=64)

        def sb(shape, dtype, name, tag=None):
            return keep.tile(shape, dtype, name=name, tag=tag or name, align_bytes=64)

        offsets = keep.tile([P, I // STRIPE], U16, name="offsets")
        nc.sync.dma_start(offsets[:], offs)
        ks_pool = sb([P, T], U8, "ks_pool")
        nc.vector.memset(ks_pool[:].bitcast(I32), 0)
        size_rows = sb([P, P], F32, "size_rows", "p_sb")
        nc.gpsimd.memset(size_rows[:], 0.0)
        vsc_columns = sb([P, PASSES, 2 * PACK], F32, "vsc_columns")
        nc.sync.dma_start(vsc_columns[:, :, 0:PACK], vsc.rearrange("(g p t) o -> p g (t o)", g=PASSES, t=PACK))
        q_raw = sb([P, PACK, Q], F32, "q_raw")
        nc.sync.dma_start(q_raw[:], query.rearrange("(p t) q -> p t q", t=PACK))
        for r in range(PACK):
            nc.sync.dma_start(
                ks_pool[r:P:QUADRANT, :].bitcast(I32), keys_scales[0, r : KP // QUADRANT : PACK, :].bitcast(I32)
            )
        kw_pool = sb([P, T], I32, "kw_pool")
        nc.sync.dma_start(kw_pool[:], keys_words[0].rearrange("p n t -> p (n t)").bitcast(I32))
        v_pool = [in_pool(b, 0, [P, T], F32, "v_pool%d" % b) for b in range(BLOCKS)]

        def load_values(b):
            nc.sync.dma_start(v_pool[b][:], vals[b * P : (b + 1) * P, :])

        mask_sb = sb([P, I], F32, "mask_sb")
        nc.sync.dma_start(mask_sb[:], mask)
        load_values(0)
        nc.sync.dma_start(size_rows[ROW0 : ROW0 + ROWS, :], size.rearrange("o (c n) -> (o c) n", n=P))
        for b in range(1, BLOCKS):
            load_values(b)

        ident = keep.tile([P, P], F32, name="ident")
        make_identity(nc, ident[:])

        def cols(g):
            return slice(g * KP, (g + 1) * KP)

        def listed(g):
            return offsets[:, g * KP // STRIPE : (g + 1) * KP // STRIPE]

        def piece(k):
            return slice(k * PIECE, (k + 1) * PIECE)

        def piece_listed(k):
            return offsets[:, k * PIECE // STRIPE : (k + 1) * PIECE // STRIPE]

        def as_pairs(row):
            return row.rearrange("e (n u h) -> e u n h", u=2, h=2)

        q_bf = sb([P, Q, PACK], BF16, "q_bf")
        nc.scalar.copy(q_bf[:], q_raw[:].rearrange("p t q -> p q t"))
        q_codes = sb([P, Q], U32, "q_codes")
        q_scales = sb([P, Q], U8, "q_scales")
        nc.vector.quantize_mx(
            out=q_codes[:].bitcast(FP8X4), scales=q_scales[:], in_=q_bf[:].rearrange("p q t -> p (q t)")
        )
        ks = sb([P, I], U8, "ks")
        nc.vector.tensor_copy(ks[:], ks_pool[:].indirect(offsets[:]))
        kw = [sb([P, PIECE], U32, "kw%d" % k) for k in range(I // PIECE)]
        for k in range(I // PIECE):
            nc.vector.tensor_copy(kw[k][:], kw_pool[:].bitcast(U32).indirect(piece_listed(k)))

        def spread(rows, name, first_bank):
            turned = psum.tile([P, P], F32, name="%s_turned" % name, tag="bank4")
            nc.tensor.transpose(turned[:], rows[:], ident[:])
            columns = sb([P, ROWS], F32, "%s_columns" % name)
            nc.scalar.copy(columns[:], turned[:, ROW0 : ROW0 + ROWS])
            banks = []
            for g in range(PASSES):
                bank = psum.tile([P, KP], F32, name="%s_ps%d" % (name, g), tag="bank%d" % (first_bank + g))
                for c in range(PACK):
                    k = g * PACK + c
                    nc.tensor.transpose(
                        bank[:, c * P : (c + 1) * P], columns[:, k : k + 1].to_broadcast([P, P]), ident[:]
                    )
                banks.append(bank)
            return banks

        vsc_ps = []
        for g in range(PASSES):
            bank = psum.tile([P, PACK, P], F32, name="vsc_ps%d" % g, tag="bank%d" % (2 + g))
            for t in range(PACK):
                nc.tensor.transpose(bank[:, t, :], vsc_columns[:, g, t : t + 1].to_broadcast([P, P]), ident[:])
            vsc_ps.append(bank)
        vsc_sb = [in_pool(BLOCKS, VSC_AT + g * 2 * HALF_ROW, [P, KP], F32, "vsc_sb%d" % g) for g in range(PASSES)]
        for g in range(PASSES):
            nc.scalar.copy(vsc_sb[g][:].rearrange("e (n t) -> e n t", t=PACK), vsc_ps[g][:].rearrange("e t n -> e n t"))

        vsc_tail = sb([P, PASSES, PIECE], F32, "vsc_tail")
        for g in range(PASSES):
            nc.scalar.copy(
                vsc_tail[:, g].rearrange("e (n t) -> e n t", t=PACK),
                vsc_ps[g][:, :, 0 : P // 2].rearrange("e t n -> e n t"),
            )

        v_codes = {}
        v_scales = {}

        def gather_scaled(b, g, scaled):
            nc.vector.tensor_tensor(scaled, v_pool[b][:].indirect(listed(g)), vsc_sb[g][:], ALU.mult)

        def gather_plain(b, g, picked):
            nc.scalar.activation(picked, v_pool[b][:].indirect(listed(g)), ACT.Copy)

        def new_pairs(b, g):
            return sb([P, 2, P, 2], BF16, "pairs%d%d" % (b, g))

        def scale_to_pairs(g, picked, pairs):
            nc.vector.tensor_tensor(pairs[:], as_pairs(picked), vsc_ps[g][:].rearrange("e (u h) n -> e u n h", h=2), ALU.mult)

        def turn_pairs(pairs, bank):
            words = pairs[:].rearrange("e u n h -> e (u n h)").bitcast(F32)
            for u in range(2):
                nc.tensor.transpose(bank[:, u, :], words[:, u * P : (u + 1) * P], ident[:])

        def turn_row(row, bank):
            words = row.bitcast(F32)
            for u in range(2):
                nc.tensor.transpose(bank[:, u, :], words[:, u : KP // 2 : 2], ident[:])

        def weave(woven, bank):
            nc.scalar.copy(woven, bank.rearrange("p g u e -> p g e u"))

        def quantize_values(b, first, woven, codes):
            count = woven.shape[1]
            scales = sb([P, count * P], U8, "v_scales%d%d" % (b, first))
            nc.vector.quantize_mx(
                out=codes.bitcast(FP8X4), scales=scales[:],
                in_=woven[:].rearrange("p g e x -> p (g e x)").bitcast(BF16),
            )
            for k in range(count):
                v_codes[b, first + k] = codes[:, k * P : (k + 1) * P]
                v_scales[b, first + k] = scales[:, k * P : (k + 1) * P]

        def round_row(rounded, scaled):
            nc.gpsimd.tensor_scalar(rounded, scaled, 1.0, 0.0, ALU.mult, ALU.add)

        def row(name, dtype=F32):
            return sb([P, KP], dtype, name)

        s_sb = sb([P, I], F32, "s_sb")
        for k, tag in enumerate(SCORE_BANKS):
            bank = psum.tile([P, PIECE], F32, name="score_ps%d" % k, tag="bank%d" % tag)
            nc.tensor.matmul_mx(
                out=bank[:], lhsT=q_codes[:].bitcast(FP8X4), lhsT_scale=q_scales[:],
                rhs=kw[k][:].bitcast(FP8X4), rhs_scale=ks[:, piece(k)], start=True, stop=True,
            )
            nc.vector.tensor_tensor(s_sb[:, piece(k)], bank[:], mask_sb[:, piece(k)], ALU.add)
        neg_max = sb([P, 1], F32, "neg_max")
        nc.vector.tensor_reduce(neg_max[:], s_sb[:], AX.X, ALU.max, negate=True)

        picked00 = row("picked00")
        gather_plain(0, 0, picked00[:])
        size_ps = spread(size_rows, "size", 0)
        p_sb = sb([P, I], F32, "p_sb")
        row_sum = sb([P, 1], F32, "row_sum")
        nc.scalar.activation(p_sb[:], s_sb[:], ACT.Exp, bias=neg_max[:], accum_out=row_sum[:])
        scaled01 = row("scaled01")
        gather_scaled(0, 1, scaled01[:])
        pairs00 = new_pairs(0, 0)
        scale_to_pairs(0, picked00[:], pairs00)
        rounded01 = row("rounded01", BF16)
        round_row(rounded01[:], scaled01[:])
        turned0 = psum.tile([P, PASSES, 2, P], F32, name="turned0", tag="bank4")
        turn_pairs(pairs00, turned0[:, 0])
        turn_row(rounded01[:], turned0[:, 1])

        inv_sum = sb([P, 1], F32, "inv_sum")
        nc.vector.reciprocal(inv_sum[:], row_sum[:])
        w_bf = sb([P, I], BF16, "w_bf")
        w_ps = [psum.tile([P, 1, 2, Q], F32, name="w_ps%d" % g, tag="bank%d" % (5 + g)) for g in range(PASSES)]
        for g in range(PASSES):
            nc.vector.scalar_tensor_tensor(
                w_bf[:, cols(g)], p_sb[:, cols(g)], inv_sum[:], size_ps[g][:], ALU.mult, ALU.mult
            )
            turn_row(w_bf[:, cols(g)], w_ps[g][:, 0])

        picked1 = [row("picked1%d" % g) for g in range(PASSES)]
        for g in range(PASSES):
            gather_plain(1, g, picked1[g][:])
        rounded10 = row("rounded10", BF16)
        nc.gpsimd.tensor_tensor(rounded10[:], picked1[0][:], vsc_sb[0][:], ALU.mult)
        pairs11 = new_pairs(1, 1)
        scale_to_pairs(1, picked1[1][:], pairs11)
        turned1 = psum.tile([P, PASSES, 2, P], F32, name="turned1", tag="bank7")
        turn_pairs(pairs11, turned1[:, 1])
        turn_row(rounded10[:], turned1[:, 0])
        woven0 = in_pool(1, 0, [P, PASSES, P, 2], F32, "woven0")
        weave(woven0[:], turned0[:])
        wt = [
            in_pool(1, HALF_ROW, [P, 1, Q, 2], F32, "wt0"),
            in_pool(BLOCKS, VSC_AT + 2 * HALF_ROW + 64 - 8 * Q, [P, 1, Q, 2], F32, "wt1"),
        ]
        weave(wt[0][:], w_ps[0][:])
        w_codes = [in_pool(LAST, 4096 + g * 4 * Q, [P, Q], U32, "w_codes%d" % g) for g in range(PASSES)]
        w_scales = [sb([P, Q], U8, "w_scales%d" % g) for g in range(PASSES)]

        def multiply(acc, b, order):
            for g in order:
                nc.tensor.matmul_mx(
                    out=acc,
                    lhsT=w_codes[g][:].bitcast(FP8X4), lhsT_scale=w_scales[g][:],
                    rhs=v_codes[b, g].bitcast(FP8X4), rhs_scale=v_scales[b, g],
                    start=(g == order[0]), stop=(g == order[-1]),
                )

        picked20 = row("picked20")
        gather_plain(2, 0, picked20[:])
        scaled21 = row("scaled21")
        gather_scaled(2, 1, scaled21[:])
        pairs20 = new_pairs(2, 0)
        scale_to_pairs(0, picked20[:], pairs20)
        rounded21 = row("rounded21", BF16)
        round_row(rounded21[:], scaled21[:])
        woven1 = in_pool(BLOCKS, VSC_AT + 2 * HALF_ROW + 64, [P, PASSES, P, 2], F32, "woven1")
        weave(woven1[:], turned1[:])
        weave(wt[1][:], w_ps[1][:])
        quantize_values(0, 0, woven0, in_pool(2, 0, [P, PASSES * P], U32, "codes0")[:])
        turned2 = psum.tile([P, PASSES, 2, P], F32, name="turned2", tag="bank4")
        turn_pairs(pairs20, turned2[:, 0])
        turn_row(rounded21[:], turned2[:, 1])

        front = [sb([P, PIECE], F32, "front3%d" % g) for g in range(PASSES)]
        back = [sb([P, PIECE], F32, "back3%d" % g) for g in range(PASSES)]
        pairs3 = [new_pairs(LAST, g) for g in range(PASSES)]
        for g in range(PASSES):
            nc.vector.tensor_tensor(
                front[g][:], v_pool[LAST][:].indirect(piece_listed(2 * g)), vsc_tail[:, g], ALU.mult
            )
            nc.scalar.activation(back[g][:], v_pool[LAST][:].indirect(piece_listed(2 * g + 1)), ACT.Copy)
        for g in range(PASSES):
            nc.vector.tensor_tensor(
                pairs3[g][:, :, P // 2 :, :],
                as_pairs(back[g][:]),
                vsc_ps[g][:, :, P // 2 :].rearrange("e (u h) n -> e u n h", h=2),
                ALU.mult,
            )
            nc.scalar.copy(pairs3[g][:, :, 0 : P // 2, :], as_pairs(front[g][:]))
        woven2 = in_pool(LAST, 0, [P, PASSES, P, 2], F32, "woven2")
        weave(woven2[:], turned2[:])
        woven3 = [sb([P, 1, P, 2], F32, "woven3%d" % g) for g in range(PASSES)]
        for g in range(PASSES):
            bank = psum.tile([P, 1, 2, P], F32, name="turned3%d" % g, tag="bank%d" % g)
            turn_pairs(pairs3[g], bank[:, 0])
            weave(woven3[g][:], bank[:])

        for g in range(PASSES):
            nc.vector.quantize_mx(
                out=w_codes[g][:].bitcast(FP8X4), scales=w_scales[g][:],
                in_=wt[g][:].rearrange("p g q u -> p (g q u)").bitcast(BF16),
            )
        quantize_values(1, 0, woven1, in_pool(LAST, HALF_ROW, [P, PASSES * P], U32, "codes1")[:])
        quantize_values(2, 0, woven2, sb([P, PASSES * P], U32, "codes2")[:])
        for g in range(PASSES):
            quantize_values(LAST, g, woven3[g], sb([P, P], U32, "codes3%d" % g)[:])
        for first, end, tag, copy in (
            (0, 2, "bank5", nc.scalar.copy),
            (2, LAST, "bank7", nc.scalar.copy),
            (LAST, BLOCKS, "bank6", nc.vector.tensor_copy),
        ):
            acc = psum.tile([P, end - first, P], F32, name="acc%d" % first, tag=tag)
            for b in range(first, end):
                multiply(acc[:, b - first], b, [0, 1])
            result = sb([P, (end - first) * P], F32, "result%d" % first)
            copy(result[:], acc[:].rearrange("p b e -> p (b e)"))
            nc.sync.dma_start(out[:, first * P : end * P], result[:])
